import numpy as np
import ml_dtypes


def mxq(x, axis, fmt="e4m3"):
    dtype, down = {"e4m3": (ml_dtypes.float8_e4m3fn, 7), "e5m2": (ml_dtypes.float8_e5m2, 14)}[fmt]
    v = np.moveaxis(np.asarray(x, np.float32).astype(ml_dtypes.bfloat16).astype(np.float64), axis, -1)
    blocks = v.reshape(v.shape[:-1] + (-1, 32))
    amax = np.abs(blocks).max(-1, keepdims=True)
    byte = np.maximum(np.where(amax > 0, np.frexp(amax)[1] - 1 + 127, 0) - down, 1)
    scale = np.exp2(byte - 127.0)
    codes = (blocks / scale).astype(np.float32).astype(dtype).astype(np.float64)
    return np.moveaxis((codes * scale).reshape(v.shape), -1, axis)


WIDE = False


def mx_kscale(k):
    if not WIDE:
        return np.ones(k)
    levels = np.array([10, -10, 5, -5, 0])
    if k % 512:
        return np.exp2(np.random.permutation(np.resize(levels, k // 32))).repeat(32)
    a = np.empty((k // 512, 16))
    for p in range(k // 512):
        a[p, :8] = np.random.permutation(np.resize(levels, 8))
        for g in range(8):
            far = levels[np.abs(levels - a[p, g]) >= 10]
            a[p, g + 8] = far[np.random.randint(len(far))]
    return np.exp2(a.ravel()).repeat(32)


def f64(x):
    return np.asarray(x).astype(np.float64)


def striped(idx):
    return np.tile(idx.reshape(-1, 16).T, (8, 1)).astype(np.uint16)


def unstriped(offs):
    return offs[:16].T.reshape(-1).astype(np.int64)


E2M1 = np.array([0.0, 0.5, 1.0, 1.5, 2.0, 3.0, 4.0, 6.0, -0.0, -0.5, -1.0, -1.5, -2.0, -3.0, -4.0, -6.0])


def pack_weight(w, fmt):
    k, n = w.shape
    w = f64(np.asarray(w, np.float32).astype(ml_dtypes.bfloat16)).reshape(k // 32, 32, n)
    amax = np.abs(w).max(1)
    if fmt == "e4m3":
        byte = np.frexp(amax)[1] - 1 + 127 - 7
    else:
        mant, ex = np.frexp(amax / 6.0)
        byte = np.where(mant > 0.5, ex, ex - 1) + 127
    byte = np.clip(np.where(amax > 0, byte, 1), 1, 254)
    scaled = (w * np.exp2(127.0 - byte)[:, None, :]).reshape(k, n).astype(np.float32)
    by_word = np.ascontiguousarray(scaled.reshape(k // 512, 128, 4, n).transpose(0, 1, 3, 2))
    if fmt == "e4m3":
        words = by_word.astype(ml_dtypes.float8_e4m3fn).view(np.uint8)
    else:
        c = by_word.astype(ml_dtypes.float4_e2m1fn).view(np.uint8) & 0xF
        words = (c[..., 0::2] | (c[..., 1::2] << 4)).reshape(k // 512, 128, 2 * n)
    return np.ascontiguousarray(words), np.ascontiguousarray(byte.astype(np.uint8).reshape(k // 512, 16, n))


def unpack_weight(words, scales, fmt):
    g, _, n = scales.shape
    words = np.ascontiguousarray(words).reshape(g, 128, n, -1)
    if fmt == "e4m3":
        vals = words.view(ml_dtypes.float8_e4m3fn).astype(np.float64)
    else:
        nib = np.empty((g, 128, n, 4), np.uint8)
        nib[..., 0::2] = words & 0xF
        nib[..., 1::2] = words >> 4
        vals = E2M1[nib]
    vals = vals * np.repeat(np.exp2(scales.astype(np.float64) - 127.0), 8, axis=1)[..., None]
    return vals.transpose(0, 1, 3, 2).reshape(g * 512, n)


K, T, E, C, N = 1536, 640, 4, 128, 1024
M = 256


def by_expert(wq, xq):
    return np.concatenate([wq[e].T @ xq[:, e * C:(e + 1) * C] for e in range(E)], axis=1)


def setup_inputs():
    n = np.random.standard_normal
    s = mx_kscale(K)[:, None]
    v = mx_kscale(N)
    w = [pack_weight(m, "e2m1") for m in n((E, K, N)) / np.sqrt(K) / s[None] * v[None, None, :]]
    x = pack_weight(n((K, T)) * s, "e4m3")
    return {
        "x_words": x[0],
        "x_scales": x[1],
        "w_words": np.stack([m[0] for m in w]),
        "w_scales": np.stack([m[1] for m in w]),
        "b": (0.3 * n((N, E)) * v[:, None]).astype(np.float32),
        "wp": (n((N, M)) / np.sqrt(N) / v[:, None]).astype(np.float32),
        "gate": np.tile(np.random.uniform(0.2, 1.0, E * C), (N, 1)).astype(np.float32),
        "offs": striped(np.random.permutation(T)[:E * C]),
    }


def reference(x_words, x_scales, w_words, w_scales, b, wp, gate, offs):
    idx = unstriped(offs)
    w = np.stack([unpack_weight(w_words[e], w_scales[e], "e2m1") for e in range(E)])
    xq = unpack_weight(x_words, x_scales, "e4m3")[:, idx]
    y = by_expert(w, xq)
    y = y + np.repeat(f64(b), C, axis=1)
    c = np.zeros((N, T))
    c[:, idx] = f64(gate) * y
    return mxq(f64(wp), 0, "e4m3").T @ mxq(c, 0, "e4m3")

@@ -1,0 +1,218 @@
+from contextlib import ExitStack
+
+import concourse.mybir as mybir
+from concourse.masks import make_identity
+
+K, T, E, C, N, M = 1536, 640, 4, 128, 1024, 256
+P = 128
+PASSES = K // 512
+HALVES = N // 512
+FT = M // P
+SEQ = 46
+SCALE_RUNS = [(0, 1), (2,), (3,)]
+
+FLOPS = 2 * K * N * E * C + 2 * N * M * T
+BYTES = 983040 + 30720 + 3145728 + 196608 + 16384 + 1048576 + 2048 + 8192 + 655360
+
+F32 = mybir.dt.float32
+BF16 = mybir.dt.bfloat16
+I32 = mybir.dt.int32
+U32 = mybir.dt.uint32
+U16 = mybir.dt.uint16
+U8 = mybir.dt.uint8
+FP8X4 = mybir.dt.float8_e4m3fn_x4
+FP4X4 = mybir.dt.float4_e2m1fn_x4
+MULT = mybir.AluOpType.mult
+ADD = mybir.AluOpType.add
+COPY = mybir.ActivationFunctionType.Copy
+
+
+def tile_moe_nxt_lin_bias_kernel(tc, x_words, x_scales, w_words, w_scales, b, wp, gate, offs, out):
+    nc = tc.nc
+    with ExitStack() as ctx:
+        keep = ctx.enter_context(tc.tile_pool(name="keep", bufs=1))
+        steps = ctx.enter_context(tc.tile_pool(name="steps", bufs=SEQ))
+        psum = ctx.enter_context(tc.psum_pool(name="psum", bufs=8))
+
+        offsets = keep.tile([P, E * C // 16], U16, name="offsets")
+        nc.sync.dma_start(offsets[:], offs)
+
+        xs = keep.tile([P, PASSES, T], U8, name="xs", align_bytes=64)
+        nc.gpsimd.memset(xs[:].rearrange("p a t -> p (a t)").bitcast(I32), 0)
+        ws = [keep.tile([P, len(run) * PASSES, N], U8, name="ws%d" % run[0], align_bytes=64) for run in SCALE_RUNS]
+        nc.vector.memset(ws[0][:].rearrange("p a n -> p (a n)").bitcast(I32), 0)
+        w_planes = {e: ws[i][:, PASSES * s : PASSES * (s + 1), :] for i, run in enumerate(SCALE_RUNS) for s, e in enumerate(run)}
+
+        ident = keep.tile([P, P], F32, name="ident")
+        make_identity(nc, ident[:])
+        for tile in ws[1:]:
+            nc.gpsimd.memset(tile[:].rearrange("p a n -> p (a n)").bitcast(I32), 0)
+        windows = [keep.tile([P, T], F32, name="window%d" % f) for f in range(FT)]
+        for f in range(FT):
+            nc.gpsimd.memset(windows[f][:].bitcast(I32), 0)
+
+        xw0 = keep.tile([P, T], I32, name="xw0")
+        xw12 = keep.tile([P, 2, T], I32, name="xw12")
+        nc.sync.dma_start(xw0[:], x_words[0].rearrange("p t r -> p (t r)").bitcast(I32))
+        xs_rows = x_scales.rearrange("a (q r) t -> r q a t", r=4)
+        for r in range(4):
+            nc.sync.dma_start(xs[r:P:32].bitcast(I32), xs_rows[r].bitcast(I32))
+        nc.sync.dma_start(xw12[:], x_words[1:3].rearrange("a p t r -> p a (t r)").bitcast(I32))
+
+        g_col = keep.tile([P, E], F32, name="g_col")
+        with nc.allow_non_contiguous_dma(reason="one gate value a partition"):
+            nc.scalar.dma_start(g_col[:], gate[0].rearrange("(e p) -> p e", p=P))
+        b_col = keep.tile([P, HALVES, 4, E], F32, name="b_col")
+        nc.scalar.dma_start(b_col[:], b.rearrange("(h p j) e -> p h j e", h=HALVES, j=4))
+
+        ww = {}
+        wp_raw = [keep.tile([P, 4, M], F32, name="wp_raw%d" % h) for h in range(HALVES)]
+
+        def load_w_scales(i):
+            rows = w_scales[SCALE_RUNS[i][0] : SCALE_RUNS[i][-1] + 1].rearrange("e a (q r) n -> r q (e a) n", r=4)
+            for r in range(4):
+                nc.sync.dma_start(ws[i][r:P:32].bitcast(I32), rows[r].bitcast(I32))
+
+        def load_w(e):
+            tile = keep.tile([P, PASSES, 2 * N], U8, name="ww%d" % e, align_bytes=64)
+            nc.sync.dma_start(tile[:].bitcast(I32), w_words[e].rearrange("a p m -> p a m").bitcast(I32))
+            for h in range(HALVES):
+                ww[e, h] = tile[:, :, 1024 * h : 1024 * (h + 1)]
+
+        def load_w_half(e, h):
+            tile = keep.tile([P, PASSES, N], U8, name="ww%d_%d" % (e, h), align_bytes=64)
+            nc.sync.dma_start(tile[:].bitcast(I32), w_words[e][:, :, 1024 * h : 1024 * (h + 1)].rearrange("a p m -> p a m").bitcast(I32))
+            ww[e, h] = tile[:]
+
+        load_w_scales(0)
+        load_w(0)
+        for h in range(HALVES):
+            nc.sync.dma_start(wp_raw[h][:], wp[512 * h : 512 * (h + 1)].rearrange("(p j) f -> p j f", j=4))
+        load_w(1)
+        load_w_scales(1)
+        load_w(2)
+        load_w_scales(2)
+        for h in range(HALVES):
+            load_w_half(3, h)
+
+        def step_tile(shape, dtype, name):
+            return steps.tile(shape, dtype, name=name, tag="step", align_bytes=64)
+
+        x_windows = [xw0[:], xw12[:, 0, :], xw12[:, 1, :]]
+        gw = {}
+        gs = {}
+
+        def gather(i):
+            lst = offsets[:, 16 * i : 16 * (i + 1)]
+            for a in range(PASSES):
+                gw[i, a] = step_tile([P, 2 * C], U32, "gw%d_%d" % (i, a))
+                nc.vector.tensor_copy(gw[i, a][:], x_windows[a].bitcast(U32).indirect(lst))
+                gs[i, a] = step_tile([P, 2 * C], U8, "gs%d_%d" % (i, a))
+                nc.vector.tensor_copy(gs[i, a][:], xs[:, a, :].indirect(lst))
+
+        gb = {}
+
+        def gated_bias(e):
+            for h in range(HALVES):
+                spread = psum.tile([P, 4, P], F32, name="spread", tag="bank")
+                for j in range(4):
+                    nc.tensor.transpose(spread[:, j, :], b_col[:, h, j, e : e + 1].to_broadcast([P, P]), ident[:])
+                gb[e, h] = keep.tile([P, P, 4], F32, name="gb%d_%d" % (e, h))
+                nc.scalar.activation(gb[e, h][:], spread[:].rearrange("s j p -> s p j"), COPY, scale=g_col[:, e : e + 1])
+
+        wp_codes = {}
+        wp_planes = {}
+
+        def quantize_wp(h):
+            grouped = keep.tile([P, M, 4], BF16, name="wp_grouped%d" % h, align_bytes=64)
+            nc.scalar.copy(grouped[:].rearrange("p (c i) j -> p c j i", i=4), wp_raw[h][:].rearrange("p j (c i) -> p c j i", i=4))
+            wp_codes[h] = step_tile([P, M], U32, "wp_codes%d" % h)
+            wp_planes[h] = keep.tile([P, M], U8, name="wp_planes%d" % h, align_bytes=64)
+            nc.vector.quantize_mx(out=wp_codes[h][:].bitcast(FP8X4), scales=wp_planes[h][:], in_=grouped[:].rearrange("p f j -> p (f j)"))
+
+        y = {}
+        c_rows = {}
+        c_grouped = {}
+        c_codes = {}
+        c_planes = {}
+        o = {}
+
+        def multiply(e, h):
+            i, s = divmod(e, 2)
+            slots = slice(s * C, (s + 1) * C)
+            y[e, h] = psum.tile([P, 512], F32, name="y", tag="bank")
+            for a in range(PASSES):
+                nc.tensor.matmul_mx(
+                    out=y[e, h][:],
+                    lhsT=gw[i, a][:, slots].bitcast(FP8X4),
+                    lhsT_scale=gs[i, a][:, slots],
+                    rhs=ww[e, h][:, a, :].bitcast(FP4X4),
+                    rhs_scale=w_planes[e][:, a, 512 * h : 512 * (h + 1)],
+                    start=(a == 0),
+                    stop=(a == PASSES - 1),
+                )
+
+        def gate_and_bias(e, h):
+            c_rows[e, h] = step_tile([P, 512], BF16, "c_rows%d_%d" % (e, h))
+            nc.vector.scalar_tensor_tensor(c_rows[e, h][:], y[e, h][:], g_col[:, e : e + 1], gb[e, h][:].rearrange("s p j -> s (p j)"), MULT, ADD)
+
+        def turn(e, h):
+            pairs = c_rows[e, h][:].bitcast(F32)
+            turned = psum.tile([P, 2, P], F32, name="turned", tag="bank")
+            for u in range(2):
+                nc.tensor.transpose(turned[:, u, :], pairs[:, u:256:2], ident[:])
+            c_grouped[e, h] = step_tile([P, C, 4], BF16, "c_grouped%d_%d" % (e, h))
+            nc.scalar.copy(c_grouped[e, h][:].bitcast(F32), turned[:].rearrange("p u s -> p s u"))
+
+        def quantize_c(e, h):
+            c_codes[e, h] = step_tile([P, C], U32, "c_codes%d_%d" % (e, h))
+            c_planes[e, h] = keep.tile([P, C], U8, name="c_planes%d_%d" % (e, h), align_bytes=64)
+            nc.vector.quantize_mx(out=c_codes[e, h][:].bitcast(FP8X4), scales=c_planes[e, h][:], in_=c_grouped[e, h][:].rearrange("p s j -> p (s j)"))
+
+        def project(e):
+            o[e] = psum.tile([P, FT, C], F32, name="o", tag="bank")
+            for f in range(FT):
+                cols = slice(f * P, (f + 1) * P)
+                for h in range(HALVES):
+                    nc.tensor.matmul_mx(
+                        out=o[e][:, f, :],
+                        lhsT=wp_codes[h][:, cols].bitcast(FP8X4),
+                        lhsT_scale=wp_planes[h][:, cols],
+                        rhs=c_codes[e, h][:].bitcast(FP8X4),
+                        rhs_scale=c_planes[e, h][:],
+                        start=(h == 0),
+                        stop=(h == HALVES - 1),
+                    )
+
+        def scatter(e, f):
+            o_slots = step_tile([P, C], F32, "o_slots%d_%d" % (e, f))
+            nc.scalar.copy(o_slots[:], o[e][:, f, :])
+            nc.vector.tensor_copy(windows[f][:].indirect(offsets[:, 8 * e : 8 * (e + 1)]), o_slots[:])
+
+        for e in range(E):
+            gated_bias(e)
+        gather(0)
+        gather(1)
+        for e in range(E):
+            for h in range(HALVES):
+                multiply(e, h)
+                gate_and_bias(e, h)
+            if e == 0:
+                quantize_wp(0)
+            else:
+                project(e - 1)
+                scatter(e - 1, 0)
+            for h in range(HALVES):
+                turn(e, h)
+            for h in range(HALVES):
+                quantize_c(e, h)
+            if e == 0:
+                quantize_wp(1)
+            else:
+                scatter(e - 1, 1)
+        project(E - 1)
+        for f in range(FT):
+            scatter(E - 1, f)
+
+        nc.sync.dma_start(out[0:P, :], windows[0][:])
+        nc.scalar.dma_start(out[P : 2 * P, :], windows[1][:])

@@ -8,8 +8,8 @@ P = 128
 PASSES = K // 512
 HALVES = N // 512
 FT = M // P
-SEQ = 46
-SCALE_RUNS = [(0, 1), (2,), (3,)]
+SEQ = 48
+LOADS = 11
 
 FLOPS = 2 * K * N * E * C + 2 * N * M * T
 BYTES = 983040 + 30720 + 3145728 + 196608 + 16384 + 1048576 + 2048 + 8192 + 655360
@@ -34,81 +34,98 @@ def tile_moe_nxt_lin_bias_kernel(tc, x_words, x_scales, w_words, w_scales, b, wp
         steps = ctx.enter_context(tc.tile_pool(name="steps", bufs=SEQ))
         psum = ctx.enter_context(tc.psum_pool(name="psum", bufs=8))
 
+        loads = ctx.enter_context(tc.tile_pool(name="loads", bufs=LOADS))
         offsets = keep.tile([P, E * C // 16], U16, name="offsets")
         nc.sync.dma_start(offsets[:], offs)
 
-        xs = keep.tile([P, PASSES, T], U8, name="xs", align_bytes=64)
-        nc.gpsimd.memset(xs[:].rearrange("p a t -> p (a t)").bitcast(I32), 0)
-        ws = [keep.tile([P, len(run) * PASSES, N], U8, name="ws%d" % run[0], align_bytes=64) for run in SCALE_RUNS]
-        nc.vector.memset(ws[0][:].rearrange("p a n -> p (a n)").bitcast(I32), 0)
-        w_planes = {e: ws[i][:, PASSES * s : PASSES * (s + 1), :] for i, run in enumerate(SCALE_RUNS) for s, e in enumerate(run)}
+        def load_tile(shape, dtype, name):
+            return loads.tile(shape, dtype, name=name, tag="load", align_bytes=64)
 
-        ident = keep.tile([P, P], F32, name="ident")
-        make_identity(nc, ident[:])
-        for tile in ws[1:]:
-            nc.gpsimd.memset(tile[:].rearrange("p a n -> p (a n)").bitcast(I32), 0)
-        windows = [keep.tile([P, T], F32, name="window%d" % f) for f in range(FT)]
-        for f in range(FT):
-            nc.gpsimd.memset(windows[f][:].bitcast(I32), 0)
+        def cleared_plane(shape, name):
+            tile = load_tile(shape, U8, name)
+            nc.vector.memset(tile[:].rearrange("p a n -> p (a n)").bitcast(I32), 0)
+            return tile
 
-        xw0 = keep.tile([P, T], I32, name="xw0")
-        xw12 = keep.tile([P, 2, T], I32, name="xw12")
-        nc.sync.dma_start(xw0[:], x_words[0].rearrange("p t r -> p (t r)").bitcast(I32))
-        xs_rows = x_scales.rearrange("a (q r) t -> r q a t", r=4)
-        for r in range(4):
-            nc.sync.dma_start(xs[r:P:32].bitcast(I32), xs_rows[r].bitcast(I32))
-        nc.sync.dma_start(xw12[:], x_words[1:3].rearrange("a p t r -> p a (t r)").bitcast(I32))
-
-        g_col = keep.tile([P, E], F32, name="g_col")
-        with nc.allow_non_contiguous_dma(reason="one gate value a partition"):
-            nc.scalar.dma_start(g_col[:], gate[0].rearrange("(e p) -> p e", p=P))
+        g_rows = keep.tile([P, C], F32, name="g_rows")
+        nc.scalar.dma_start(g_rows[:], gate.rearrange("r (e s) -> (r e) s", s=C)[0:P])
         b_col = keep.tile([P, HALVES, 4, E], F32, name="b_col")
         nc.scalar.dma_start(b_col[:], b.rearrange("(h p j) e -> p h j e", h=HALVES, j=4))
 
+        ident = keep.tile([P, P], F32, name="ident")
+        make_identity(nc, ident[:])
+
+        xw0 = keep.tile([P, T], I32, name="xw0")
+        nc.sync.dma_start(xw0[:], x_words[0].rearrange("p t r -> p (t r)").bitcast(I32))
+        xs = cleared_plane([P, PASSES, T], "xs")
+        xs_rows = x_scales.rearrange("a (q r) t -> r q a t", r=4)
+        for r in range(4):
+            nc.sync.dma_start(xs[r:P:32].bitcast(I32), xs_rows[r].bitcast(I32))
+        ws = [cleared_plane([P, 2 * PASSES, N], "ws0")]
+        zero = keep.tile([P, 8], F32, name="zero")
+        nc.vector.memset(zero[:], 0.0)
+        xw12 = load_tile([P, 2, T], I32, "xw12")
+        nc.sync.dma_start(xw12[:], x_words[1:3].rearrange("a p t r -> p a (t r)").bitcast(I32))
+        x_windows = [xw0[:], xw12[:, 0, :], xw12[:, 1, :]]
+        ws.append(keep.tile([P, 2 * PASSES, N], U8, name="ws1", align_bytes=64))
+        nc.vector.memset(ws[1][:].rearrange("p a n -> p (a n)").bitcast(I32), 0)
+        w_planes = {e: ws[e // 2][:, PASSES * (e % 2) : PASSES * (e % 2 + 1), :] for e in range(E)}
+
+        windows = [keep.tile([P, T], F32, name="window%d" % f) for f in range(FT)]
+        for f in range(FT):
+            nc.scalar.activation(windows[f][:], zero[:, 0:1].to_broadcast([P, T]), COPY)
+
         ww = {}
-        wp_raw = [keep.tile([P, 4, M], F32, name="wp_raw%d" % h) for h in range(HALVES)]
+        wp_raw = {}
 
         def load_w_scales(i):
-            rows = w_scales[SCALE_RUNS[i][0] : SCALE_RUNS[i][-1] + 1].rearrange("e a (q r) n -> r q (e a) n", r=4)
+            rows = w_scales[2 * i : 2 * i + 2].rearrange("e a (q r) n -> r q (e a) n", r=4)
             for r in range(4):
                 nc.sync.dma_start(ws[i][r:P:32].bitcast(I32), rows[r].bitcast(I32))
 
         def load_w(e):
-            tile = keep.tile([P, PASSES, 2 * N], U8, name="ww%d" % e, align_bytes=64)
+            tile = load_tile([P, PASSES, 2 * N], U8, "ww%d" % e)
             nc.sync.dma_start(tile[:].bitcast(I32), w_words[e].rearrange("a p m -> p a m").bitcast(I32))
             for h in range(HALVES):
                 ww[e, h] = tile[:, :, 1024 * h : 1024 * (h + 1)]
 
         def load_w_half(e, h):
-            tile = keep.tile([P, PASSES, N], U8, name="ww%d_%d" % (e, h), align_bytes=64)
+            tile = load_tile([P, PASSES, N], U8, "ww%d_%d" % (e, h))
             nc.sync.dma_start(tile[:].bitcast(I32), w_words[e][:, :, 1024 * h : 1024 * (h + 1)].rearrange("a p m -> p a m").bitcast(I32))
             ww[e, h] = tile[:]
 
-        load_w_scales(0)
-        load_w(0)
-        for h in range(HALVES):
+        def load_wp(h):
+            wp_raw[h] = load_tile([P, 4, M], F32, "wp_raw%d" % h)
             nc.sync.dma_start(wp_raw[h][:], wp[512 * h : 512 * (h + 1)].rearrange("(p j) f -> p j f", j=4))
+
+        load_w_half(0, 0)
+        load_w_scales(0)
+        load_w_half(0, 1)
+        load_wp(0)
         load_w(1)
+        load_wp(1)
         load_w_scales(1)
         load_w(2)
-        load_w_scales(2)
         for h in range(HALVES):
             load_w_half(3, h)
+
+        g_turned = psum.tile([P, C], F32, name="g_turned", tag="bank")
+        nc.tensor.transpose(g_turned[:], g_rows[:], ident[:])
+        g_col = keep.tile([P, E], F32, name="g_col")
+        nc.scalar.copy(g_col[:], g_turned[:, 0:E])
 
         def step_tile(shape, dtype, name):
             return steps.tile(shape, dtype, name=name, tag="step", align_bytes=64)
 
-        x_windows = [xw0[:], xw12[:, 0, :], xw12[:, 1, :]]
         gw = {}
         gs = {}
 
-        def gather(i):
-            lst = offsets[:, 16 * i : 16 * (i + 1)]
-            for a in range(PASSES):
-                gw[i, a] = step_tile([P, 2 * C], U32, "gw%d_%d" % (i, a))
-                nc.vector.tensor_copy(gw[i, a][:], x_windows[a].bitcast(U32).indirect(lst))
-                gs[i, a] = step_tile([P, 2 * C], U8, "gs%d_%d" % (i, a))
-                nc.vector.tensor_copy(gs[i, a][:], xs[:, a, :].indirect(lst))
+        def gather_scales(i, a):
+            gs[i, a] = step_tile([P, 2 * C], U8, "gs%d_%d" % (i, a))
+            nc.vector.tensor_copy(gs[i, a][:], xs[:, a, :].indirect(offsets[:, 16 * i : 16 * (i + 1)]))
+
+        def gather_words(i, a):
+            gw[i, a] = step_tile([P, 2 * C], U32, "gw%d_%d" % (i, a))
+            nc.vector.tensor_copy(gw[i, a][:], x_windows[a].bitcast(U32).indirect(offsets[:, 16 * i : 16 * (i + 1)]))
 
         gb = {}
 
@@ -123,9 +140,14 @@ def tile_moe_nxt_lin_bias_kernel(tc, x_words, x_scales, w_words, w_scales, b, wp
         wp_codes = {}
         wp_planes = {}
 
+        wp_grouped = {}
+
+        def group_wp(h):
+            wp_grouped[h] = step_tile([P, M, 4], BF16, "wp_grouped%d" % h)
+            nc.scalar.copy(wp_grouped[h][:].rearrange("p (c i) j -> p c j i", i=4), wp_raw[h][:].rearrange("p j (c i) -> p c j i", i=4))
+
         def quantize_wp(h):
-            grouped = keep.tile([P, M, 4], BF16, name="wp_grouped%d" % h, align_bytes=64)
-            nc.scalar.copy(grouped[:].rearrange("p (c i) j -> p c j i", i=4), wp_raw[h][:].rearrange("p j (c i) -> p c j i", i=4))
+            grouped = wp_grouped[h]
             wp_codes[h] = step_tile([P, M], U32, "wp_codes%d" % h)
             wp_planes[h] = keep.tile([P, M], U8, name="wp_planes%d" % h, align_bytes=64)
             nc.vector.quantize_mx(out=wp_codes[h][:].bitcast(FP8X4), scales=wp_planes[h][:], in_=grouped[:].rearrange("p f j -> p (f j)"))
@@ -189,27 +211,57 @@ def tile_moe_nxt_lin_bias_kernel(tc, x_words, x_scales, w_words, w_scales, b, wp
             nc.scalar.copy(o_slots[:], o[e][:, f, :])
             nc.vector.tensor_copy(windows[f][:].indirect(offsets[:, 8 * e : 8 * (e + 1)]), o_slots[:])
 
-        for e in range(E):
+        for e in range(2):
             gated_bias(e)
-        gather(0)
-        gather(1)
-        for e in range(E):
+        gather_words(0, 0)
+        for a in range(PASSES):
+            gather_scales(0, a)
+        for a in range(1, PASSES):
+            gather_words(0, a)
+
+        gather_scales(1, 0)
+        gather_scales(1, 1)
+        multiply(0, 0)
+        gate_and_bias(0, 0)
+        gather_scales(1, 2)
+        multiply(0, 1)
+        gated_bias(2)
+        gate_and_bias(0, 1)
+        gather_words(1, 0)
+        turn(0, 0)
+        group_wp(0)
+        turn(0, 1)
+        gated_bias(E - 1)
+        gather_words(1, 1)
+        quantize_c(0, 0)
+        quantize_wp(0)
+        quantize_c(0, 1)
+        gather_words(1, 2)
+        group_wp(1)
+
+        for h in range(HALVES):
+            multiply(1, h)
+            gate_and_bias(1, h)
+        for h in range(HALVES):
+            turn(1, h)
+        quantize_wp(1)
+        for h in range(HALVES):
+            quantize_c(1, h)
+        project(0)
+        for f in range(FT):
+            scatter(0, f)
+
+        for e in range(2, E):
             for h in range(HALVES):
                 multiply(e, h)
                 gate_and_bias(e, h)
-            if e == 0:
-                quantize_wp(0)
-            else:
-                project(e - 1)
-                scatter(e - 1, 0)
+            project(e - 1)
+            scatter(e - 1, 0)
             for h in range(HALVES):
                 turn(e, h)
             for h in range(HALVES):
                 quantize_c(e, h)
-            if e == 0:
-                quantize_wp(1)
-            else:
-                scatter(e - 1, 1)
+            scatter(e - 1, 1)
         project(E - 1)
         for f in range(FT):
             scatter(E - 1, f)

@@ -9,7 +9,8 @@ PASSES = K // 512
 HALVES = N // 512
 FT = M // P
 SEQ = 48
-LOADS = 11
+LOADS = 10
+SCALE_RUNS = [(0, 1), (2,), (3,)]
 
 FLOPS = 2 * K * N * E * C + 2 * N * M * T
 BYTES = 983040 + 30720 + 3145728 + 196608 + 16384 + 1048576 + 2048 + 8192 + 655360
@@ -66,9 +67,10 @@ def tile_moe_nxt_lin_bias_kernel(tc, x_words, x_scales, w_words, w_scales, b, wp
         xw12 = load_tile([P, 2, T], I32, "xw12")
         nc.sync.dma_start(xw12[:], x_words[1:3].rearrange("a p t r -> p a (t r)").bitcast(I32))
         x_windows = [xw0[:], xw12[:, 0, :], xw12[:, 1, :]]
-        ws.append(keep.tile([P, 2 * PASSES, N], U8, name="ws1", align_bytes=64))
-        nc.vector.memset(ws[1][:].rearrange("p a n -> p (a n)").bitcast(I32), 0)
-        w_planes = {e: ws[e // 2][:, PASSES * (e % 2) : PASSES * (e % 2 + 1), :] for e in range(E)}
+        for i in range(1, len(SCALE_RUNS)):
+            ws.append(keep.tile([P, PASSES, N], U8, name="ws%d" % i, align_bytes=64))
+            nc.vector.memset(ws[i][:].rearrange("p a n -> p (a n)").bitcast(I32), 0)
+        w_planes = {e: ws[i][:, PASSES * s : PASSES * (s + 1), :] for i, run in enumerate(SCALE_RUNS) for s, e in enumerate(run)}
 
         windows = [keep.tile([P, T], F32, name="window%d" % f) for f in range(FT)]
         for f in range(FT):
@@ -78,7 +80,7 @@ def tile_moe_nxt_lin_bias_kernel(tc, x_words, x_scales, w_words, w_scales, b, wp
         wp_raw = {}
 
         def load_w_scales(i):
-            rows = w_scales[2 * i : 2 * i + 2].rearrange("e a (q r) n -> r q (e a) n", r=4)
+            rows = w_scales[SCALE_RUNS[i][0] : SCALE_RUNS[i][-1] + 1].rearrange("e a (q r) n -> r q (e a) n", r=4)
             for r in range(4):
                 nc.sync.dma_start(ws[i][r:P:32].bitcast(I32), rows[r].bitcast(I32))
 
@@ -97,14 +99,14 @@ def tile_moe_nxt_lin_bias_kernel(tc, x_words, x_scales, w_words, w_scales, b, wp
             wp_raw[h] = load_tile([P, 4, M], F32, "wp_raw%d" % h)
             nc.sync.dma_start(wp_raw[h][:], wp[512 * h : 512 * (h + 1)].rearrange("(p j) f -> p j f", j=4))
 
-        load_w_half(0, 0)
         load_w_scales(0)
-        load_w_half(0, 1)
-        load_wp(0)
+        load_w(0)
         load_w(1)
-        load_wp(1)
+        for h in range(HALVES):
+            load_wp(h)
         load_w_scales(1)
         load_w(2)
+        load_w_scales(2)
         for h in range(HALVES):
             load_w_half(3, h)
 
@@ -211,57 +213,37 @@ def tile_moe_nxt_lin_bias_kernel(tc, x_words, x_scales, w_words, w_scales, b, wp
             nc.scalar.copy(o_slots[:], o[e][:, f, :])
             nc.vector.tensor_copy(windows[f][:].indirect(offsets[:, 8 * e : 8 * (e + 1)]), o_slots[:])
 
-        for e in range(2):
+        for e in range(E):
             gated_bias(e)
         gather_words(0, 0)
         for a in range(PASSES):
             gather_scales(0, a)
         for a in range(1, PASSES):
             gather_words(0, a)
+        for a in range(PASSES):
+            gather_scales(1, a)
 
-        gather_scales(1, 0)
-        gather_scales(1, 1)
-        multiply(0, 0)
-        gate_and_bias(0, 0)
-        gather_scales(1, 2)
-        multiply(0, 1)
-        gated_bias(2)
-        gate_and_bias(0, 1)
-        gather_words(1, 0)
-        turn(0, 0)
-        group_wp(0)
-        turn(0, 1)
-        gated_bias(E - 1)
-        gather_words(1, 1)
-        quantize_c(0, 0)
-        quantize_wp(0)
-        quantize_c(0, 1)
-        gather_words(1, 2)
-        group_wp(1)
-
-        for h in range(HALVES):
-            multiply(1, h)
-            gate_and_bias(1, h)
-        for h in range(HALVES):
-            turn(1, h)
-        quantize_wp(1)
-        for h in range(HALVES):
-            quantize_c(1, h)
-        project(0)
-        for f in range(FT):
-            scatter(0, f)
-
-        for e in range(2, E):
-            for h in range(HALVES):
-                multiply(e, h)
-                gate_and_bias(e, h)
-            project(e - 1)
-            scatter(e - 1, 0)
-            for h in range(HALVES):
-                turn(e, h)
-            for h in range(HALVES):
-                quantize_c(e, h)
-            scatter(e - 1, 1)
+        units = [(e, h) for e in range(E) for h in range(HALVES)]
+        multiply(*units[0])
+        for u, (e, h) in enumerate(units):
+            if u + 1 < len(units):
+                multiply(*units[u + 1])
+            gate_and_bias(e, h)
+            if u > 0:
+                quantize_c(*units[u - 1])
+            turn(e, h)
+            if u < PASSES:
+                gather_words(1, u)
+            if u in (0, 1):
+                group_wp(u)
+            if u in (1, 2):
+                quantize_wp(u - 1)
+            if h == 0 and e > 0:
+                project(e - 1)
+            if u >= 3:
+                scatter(*units[u - 3])
+        quantize_c(*units[-1])
+        scatter(*units[-3])
         project(E - 1)
         for f in range(FT):
             scatter(E - 1, f)

@@ -10,7 +10,7 @@ HALVES = N // 512
 FT = M // P
 SEQ = 48
 LOADS = 10
-SCALE_RUNS = [(0, 1), (2,), (3,)]
+SCALE_RUNS = [(0, 1), (2, 3)]
 
 FLOPS = 2 * K * N * E * C + 2 * N * M * T
 BYTES = 983040 + 30720 + 3145728 + 196608 + 16384 + 1048576 + 2048 + 8192 + 655360
@@ -48,41 +48,31 @@ def tile_moe_nxt_lin_bias_kernel(tc, x_words, x_scales, w_words, w_scales, b, wp
             return tile
 
         g_rows = keep.tile([P, C], F32, name="g_rows")
-        nc.scalar.dma_start(g_rows[:], gate.rearrange("r (e s) -> (r e) s", s=C)[0:P])
+        nc.gpsimd.dma_start(g_rows[:], gate.rearrange("r (e s) -> (r e) s", s=C)[0:P])
         b_col = keep.tile([P, HALVES, 4, E], F32, name="b_col")
         nc.scalar.dma_start(b_col[:], b.rearrange("(h p j) e -> p h j e", h=HALVES, j=4))
 
         ident = keep.tile([P, P], F32, name="ident")
         make_identity(nc, ident[:])
 
-        xw0 = keep.tile([P, T], I32, name="xw0")
-        nc.sync.dma_start(xw0[:], x_words[0].rearrange("p t r -> p (t r)").bitcast(I32))
         xs = cleared_plane([P, PASSES, T], "xs")
         xs_rows = x_scales.rearrange("a (q r) t -> r q a t", r=4)
         for r in range(4):
-            nc.sync.dma_start(xs[r:P:32].bitcast(I32), xs_rows[r].bitcast(I32))
+            nc.scalar.dma_start(xs[r:P:32].bitcast(I32), xs_rows[r].bitcast(I32))
+        windows = [keep.tile([P, T], F32, name="window0")]
+        nc.vector.memset(windows[0][:].bitcast(I32), 0)
         ws = [cleared_plane([P, 2 * PASSES, N], "ws0")]
-        zero = keep.tile([P, 8], F32, name="zero")
-        nc.vector.memset(zero[:], 0.0)
-        xw12 = load_tile([P, 2, T], I32, "xw12")
-        nc.sync.dma_start(xw12[:], x_words[1:3].rearrange("a p t r -> p a (t r)").bitcast(I32))
-        x_windows = [xw0[:], xw12[:, 0, :], xw12[:, 1, :]]
-        for i in range(1, len(SCALE_RUNS)):
-            ws.append(keep.tile([P, PASSES, N], U8, name="ws%d" % i, align_bytes=64))
-            nc.vector.memset(ws[i][:].rearrange("p a n -> p (a n)").bitcast(I32), 0)
-        w_planes = {e: ws[i][:, PASSES * s : PASSES * (s + 1), :] for i, run in enumerate(SCALE_RUNS) for s, e in enumerate(run)}
-
-        windows = [keep.tile([P, T], F32, name="window%d" % f) for f in range(FT)]
-        for f in range(FT):
-            nc.scalar.activation(windows[f][:], zero[:, 0:1].to_broadcast([P, T]), COPY)
+        xw = load_tile([P, PASSES, T], I32, "xw")
+        nc.sync.dma_start(xw[:], x_words.rearrange("a p t r -> p a (t r)").bitcast(I32))
+        x_windows = [xw[:, a, :] for a in range(PASSES)]
 
         ww = {}
         wp_raw = {}
 
-        def load_w_scales(i):
+        def load_w_scales(i, queue):
             rows = w_scales[SCALE_RUNS[i][0] : SCALE_RUNS[i][-1] + 1].rearrange("e a (q r) n -> r q (e a) n", r=4)
             for r in range(4):
-                nc.sync.dma_start(ws[i][r:P:32].bitcast(I32), rows[r].bitcast(I32))
+                queue.dma_start(ws[i][r:P:32].bitcast(I32), rows[r].bitcast(I32))
 
         def load_w(e):
             tile = load_tile([P, PASSES, 2 * N], U8, "ww%d" % e)
@@ -95,25 +85,32 @@ def tile_moe_nxt_lin_bias_kernel(tc, x_words, x_scales, w_words, w_scales, b, wp
             nc.sync.dma_start(tile[:].bitcast(I32), w_words[e][:, :, 1024 * h : 1024 * (h + 1)].rearrange("a p m -> p a m").bitcast(I32))
             ww[e, h] = tile[:]
 
-        def load_wp(h):
-            wp_raw[h] = load_tile([P, 4, M], F32, "wp_raw%d" % h)
-            nc.sync.dma_start(wp_raw[h][:], wp[512 * h : 512 * (h + 1)].rearrange("(p j) f -> p j f", j=4))
+        def load_wp():
+            tile = load_tile([P, HALVES, 4 * M], F32, "wp_raw")
+            nc.sync.dma_start(tile[:], wp.rearrange("(h p j) f -> p h (j f)", h=HALVES, j=4))
+            for h in range(HALVES):
+                wp_raw[h] = tile[:, h, :].rearrange("p (j f) -> p j f", j=4)
 
-        load_w_scales(0)
         load_w(0)
+        load_w_scales(0, nc.scalar)
+        ws.append(keep.tile([P, 2 * PASSES, N], U8, name="ws1", align_bytes=64))
+        nc.vector.memset(ws[1][:].rearrange("p a n -> p (a n)").bitcast(I32), 0)
+        w_planes = {e: ws[i][:, PASSES * s : PASSES * (s + 1), :] for i, run in enumerate(SCALE_RUNS) for s, e in enumerate(run)}
+        windows.append(load_tile([P, T], F32, "window1"))
+        nc.vector.memset(windows[1][:].bitcast(I32), 0)
         load_w(1)
-        for h in range(HALVES):
-            load_wp(h)
-        load_w_scales(1)
+        load_wp()
+        load_w_scales(1, nc.sync)
         load_w(2)
-        load_w_scales(2)
         for h in range(HALVES):
             load_w_half(3, h)
 
-        g_turned = psum.tile([P, C], F32, name="g_turned", tag="bank")
-        nc.tensor.transpose(g_turned[:], g_rows[:], ident[:])
         g_col = keep.tile([P, E], F32, name="g_col")
-        nc.scalar.copy(g_col[:], g_turned[:, 0:E])
+
+        def turn_gate():
+            g_turned = psum.tile([P, C], F32, name="g_turned", tag="bank")
+            nc.tensor.transpose(g_turned[:], g_rows[:], ident[:])
+            nc.scalar.copy(g_col[:], g_turned[:, 0:E])
 
         def step_tile(shape, dtype, name):
             return steps.tile(shape, dtype, name=name, tag="step", align_bytes=64)
@@ -131,13 +128,18 @@ def tile_moe_nxt_lin_bias_kernel(tc, x_words, x_scales, w_words, w_scales, b, wp
 
         gb = {}
 
+        spread = {}
+
+        def spread_bias(e):
+            for h in range(HALVES):
+                spread[e, h] = psum.tile([P, 4, P], F32, name="spread", tag="bank")
+                for j in range(4):
+                    nc.tensor.transpose(spread[e, h][:, j, :], b_col[:, h, j, e : e + 1].to_broadcast([P, P]), ident[:])
+
         def gated_bias(e):
             for h in range(HALVES):
-                spread = psum.tile([P, 4, P], F32, name="spread", tag="bank")
-                for j in range(4):
-                    nc.tensor.transpose(spread[:, j, :], b_col[:, h, j, e : e + 1].to_broadcast([P, P]), ident[:])
                 gb[e, h] = keep.tile([P, P, 4], F32, name="gb%d_%d" % (e, h))
-                nc.scalar.activation(gb[e, h][:], spread[:].rearrange("s j p -> s p j"), COPY, scale=g_col[:, e : e + 1])
+                nc.scalar.activation(gb[e, h][:], spread[e, h][:].rearrange("s j p -> s p j"), COPY, scale=g_col[:, e : e + 1])
 
         wp_codes = {}
         wp_planes = {}
@@ -146,7 +148,7 @@ def tile_moe_nxt_lin_bias_kernel(tc, x_words, x_scales, w_words, w_scales, b, wp
 
         def group_wp(h):
             wp_grouped[h] = step_tile([P, M, 4], BF16, "wp_grouped%d" % h)
-            nc.scalar.copy(wp_grouped[h][:].rearrange("p (c i) j -> p c j i", i=4), wp_raw[h][:].rearrange("p j (c i) -> p c j i", i=4))
+            nc.scalar.copy(wp_grouped[h][:].rearrange("p (c i) j -> p c j i", i=4), wp_raw[h].rearrange("p j (c i) -> p c j i", i=4))
 
         def quantize_wp(h):
             grouped = wp_grouped[h]
@@ -213,40 +215,65 @@ def tile_moe_nxt_lin_bias_kernel(tc, x_words, x_scales, w_words, w_scales, b, wp
             nc.scalar.copy(o_slots[:], o[e][:, f, :])
             nc.vector.tensor_copy(windows[f][:].indirect(offsets[:, 8 * e : 8 * (e + 1)]), o_slots[:])
 
-        for e in range(E):
+        for e in range(2):
+            spread_bias(e)
+        turn_gate()
+        for e in range(2):
             gated_bias(e)
-        gather_words(0, 0)
+        for e in range(2, E):
+            spread_bias(e)
+            gated_bias(e)
         for a in range(PASSES):
             gather_scales(0, a)
-        for a in range(1, PASSES):
-            gather_words(0, a)
+        gather_scales(1, 0)
         for a in range(PASSES):
+            gather_words(0, a)
+        for a in range(1, PASSES):
             gather_scales(1, a)
+        for a in range(PASSES - 1):
+            gather_words(1, a)
 
-        units = [(e, h) for e in range(E) for h in range(HALVES)]
-        multiply(*units[0])
-        for u, (e, h) in enumerate(units):
-            if u + 1 < len(units):
-                multiply(*units[u + 1])
-            gate_and_bias(e, h)
-            if u > 0:
-                quantize_c(*units[u - 1])
-            turn(e, h)
-            if u < PASSES:
-                gather_words(1, u)
-            if u in (0, 1):
-                group_wp(u)
-            if u in (1, 2):
-                quantize_wp(u - 1)
-            if h == 0 and e > 0:
-                project(e - 1)
-            if u >= 3:
-                scatter(*units[u - 3])
-        quantize_c(*units[-1])
-        scatter(*units[-3])
-        project(E - 1)
+        gather_words(1, PASSES - 1)
+
+        def expert_products(e):
+            for h in range(HALVES):
+                multiply(e, h)
+                gate_and_bias(e, h)
+
+        def expert_codes(e):
+            for h in range(HALVES):
+                turn(e, h)
+            for h in range(HALVES):
+                quantize_c(e, h)
+
+        expert_products(0)
+        group_wp(0)
+        expert_products(1)
+        quantize_wp(0)
+        expert_codes(0)
+        group_wp(1)
+
+        multiply(2, 0)
+        gate_and_bias(2, 0)
+        quantize_wp(1)
+        multiply(2, 1)
+        gate_and_bias(2, 1)
+        expert_codes(1)
+        project(0)
         for f in range(FT):
-            scatter(E - 1, f)
+            scatter(0, f)
+
+        expert_products(3)
+        expert_codes(2)
+        project(1)
+        scatter(1, 0)
+        expert_codes(3)
+        scatter(1, 1)
+        for e in range(2, E):
+            project(e)
+        for e in range(2, E):
+            for f in range(FT):
+                scatter(e, f)
 
         nc.sync.dma_start(out[0:P, :], windows[0][:])
         nc.scalar.dma_start(out[P : 2 * P, :], windows[1][:])

@@ -9,7 +9,8 @@ PASSES = K // 512
 HALVES = N // 512
 FT = M // P
 SEQ = 48
-LOADS = 10
+LOADS = 9
+ON_SCALAR = [(1, 0), (2, 0), (3, 0)]
 SCALE_RUNS = [(0, 1), (2, 3)]
 
 FLOPS = 2 * K * N * E * C + 2 * N * M * T
@@ -47,6 +48,8 @@ def tile_moe_nxt_lin_bias_kernel(tc, x_words, x_scales, w_words, w_scales, b, wp
             nc.vector.memset(tile[:].rearrange("p a n -> p (a n)").bitcast(I32), 0)
             return tile
 
+        xs = keep.tile([P, PASSES, T], U8, name="xs", align_bytes=64)
+        nc.gpsimd.memset(xs[:].rearrange("p a t -> p (a t)").bitcast(I32), 0)
         g_rows = keep.tile([P, C], F32, name="g_rows")
         nc.gpsimd.dma_start(g_rows[:], gate.rearrange("r (e s) -> (r e) s", s=C)[0:P])
         b_col = keep.tile([P, HALVES, 4, E], F32, name="b_col")
@@ -55,24 +58,26 @@ def tile_moe_nxt_lin_bias_kernel(tc, x_words, x_scales, w_words, w_scales, b, wp
         ident = keep.tile([P, P], F32, name="ident")
         make_identity(nc, ident[:])
 
-        xs = cleared_plane([P, PASSES, T], "xs")
+        xw0 = keep.tile([P, T], I32, name="xw0")
+        nc.sync.dma_start(xw0[:], x_words[0].rearrange("p t r -> p (t r)").bitcast(I32))
         xs_rows = x_scales.rearrange("a (q r) t -> r q a t", r=4)
         for r in range(4):
             nc.scalar.dma_start(xs[r:P:32].bitcast(I32), xs_rows[r].bitcast(I32))
-        windows = [keep.tile([P, T], F32, name="window0")]
+        windows = [keep.tile([P, T], F32, name="window%d" % f) for f in range(FT)]
         nc.vector.memset(windows[0][:].bitcast(I32), 0)
         ws = [cleared_plane([P, 2 * PASSES, N], "ws0")]
-        xw = load_tile([P, PASSES, T], I32, "xw")
-        nc.sync.dma_start(xw[:], x_words.rearrange("a p t r -> p a (t r)").bitcast(I32))
-        x_windows = [xw[:, a, :] for a in range(PASSES)]
+        nc.vector.memset(windows[1][:].bitcast(I32), 0)
+        xw12 = load_tile([P, 2, T], I32, "xw12")
+        nc.sync.dma_start(xw12[:], x_words[1:3].rearrange("a p t r -> p a (t r)").bitcast(I32))
+        x_windows = [xw0[:], xw12[:, 0, :], xw12[:, 1, :]]
 
         ww = {}
         wp_raw = {}
 
-        def load_w_scales(i, queue):
+        def load_w_scales(i):
             rows = w_scales[SCALE_RUNS[i][0] : SCALE_RUNS[i][-1] + 1].rearrange("e a (q r) n -> r q (e a) n", r=4)
             for r in range(4):
-                queue.dma_start(ws[i][r:P:32].bitcast(I32), rows[r].bitcast(I32))
+                nc.sync.dma_start(ws[i][r:P:32].bitcast(I32), rows[r].bitcast(I32))
 
         def load_w(e):
             tile = load_tile([P, PASSES, 2 * N], U8, "ww%d" % e)
@@ -92,15 +97,13 @@ def tile_moe_nxt_lin_bias_kernel(tc, x_words, x_scales, w_words, w_scales, b, wp
                 wp_raw[h] = tile[:, h, :].rearrange("p (j f) -> p j f", j=4)
 
         load_w(0)
-        load_w_scales(0, nc.scalar)
-        ws.append(keep.tile([P, 2 * PASSES, N], U8, name="ws1", align_bytes=64))
+        load_w_scales(0)
+        ws.append(load_tile([P, 2 * PASSES, N], U8, "ws1"))
         nc.vector.memset(ws[1][:].rearrange("p a n -> p (a n)").bitcast(I32), 0)
         w_planes = {e: ws[i][:, PASSES * s : PASSES * (s + 1), :] for i, run in enumerate(SCALE_RUNS) for s, e in enumerate(run)}
-        windows.append(load_tile([P, T], F32, "window1"))
-        nc.vector.memset(windows[1][:].bitcast(I32), 0)
         load_w(1)
         load_wp()
-        load_w_scales(1, nc.sync)
+        load_w_scales(1)
         load_w(2)
         for h in range(HALVES):
             load_w_half(3, h)
@@ -138,8 +141,11 @@ def tile_moe_nxt_lin_bias_kernel(tc, x_words, x_scales, w_words, w_scales, b, wp
 
         def gated_bias(e):
             for h in range(HALVES):
-                gb[e, h] = keep.tile([P, P, 4], F32, name="gb%d_%d" % (e, h))
-                nc.scalar.activation(gb[e, h][:], spread[e, h][:].rearrange("s j p -> s p j"), COPY, scale=g_col[:, e : e + 1])
+                gb[e, h] = keep.tile([P, 512], F32, name="gb%d_%d" % (e, h))
+                if (e, h) in ON_SCALAR:
+                    nc.scalar.activation(gb[e, h][:], spread[e, h][:].rearrange("s j p -> s (j p)"), COPY, scale=g_col[:, e : e + 1])
+                else:
+                    nc.scalar.activation(gb[e, h][:].rearrange("s (p j) -> s p j", j=4), spread[e, h][:].rearrange("s j p -> s p j"), COPY, scale=g_col[:, e : e + 1])
 
         wp_codes = {}
         wp_planes = {}
@@ -179,10 +185,23 @@ def tile_moe_nxt_lin_bias_kernel(tc, x_words, x_scales, w_words, w_scales, b, wp
                 )
 
         def gate_and_bias(e, h):
+            if (e, h) in ON_SCALAR:
+                c_rows[e, h] = step_tile([P, 4, P], F32, "gated%d_%d" % (e, h))
+                nc.scalar.activation(c_rows[e, h][:], y[e, h][:].rearrange("s (p j) -> s j p", j=4), COPY, scale=g_col[:, e : e + 1])
+                return
             c_rows[e, h] = step_tile([P, 512], BF16, "c_rows%d_%d" % (e, h))
-            nc.vector.scalar_tensor_tensor(c_rows[e, h][:], y[e, h][:], g_col[:, e : e + 1], gb[e, h][:].rearrange("s p j -> s (p j)"), MULT, ADD)
+            nc.vector.scalar_tensor_tensor(c_rows[e, h][:], y[e, h][:], g_col[:, e : e + 1], gb[e, h][:], MULT, ADD)
 
         def turn(e, h):
+            if (e, h) in ON_SCALAR:
+                summed = psum.tile([P, 4, P], F32, name="summed", tag="bank")
+                for j in range(4):
+                    nc.tensor.matmul(summed[:, j, :], gb[e, h][:, P * j : P * (j + 1)], ident[:], is_transpose=True, start=(j == 0), stop=False)
+                for j in range(4):
+                    nc.tensor.matmul(summed[:, j, :], c_rows[e, h][:, j, :], ident[:], is_transpose=True, start=False, stop=(j == 3))
+                c_grouped[e, h] = step_tile([P, C, 4], BF16, "c_grouped%d_%d" % (e, h))
+                nc.scalar.copy(c_grouped[e, h][:], summed[:].rearrange("p j s -> p s j"))
+                return
             pairs = c_rows[e, h][:].bitcast(F32)
             turned = psum.tile([P, 2, P], F32, name="turned", tag="bank")
             for u in range(2):
@@ -223,17 +242,15 @@ def tile_moe_nxt_lin_bias_kernel(tc, x_words, x_scales, w_words, w_scales, b, wp
         for e in range(2, E):
             spread_bias(e)
             gated_bias(e)
+        gather_words(0, 0)
         for a in range(PASSES):
             gather_scales(0, a)
-        gather_scales(1, 0)
-        for a in range(PASSES):
-            gather_words(0, a)
         for a in range(1, PASSES):
+            gather_words(0, a)
+        for a in range(PASSES):
             gather_scales(1, a)
         for a in range(PASSES - 1):
             gather_words(1, a)
-
-        gather_words(1, PASSES - 1)
 
         def expert_products(e):
             for h in range(HALVES):
@@ -248,6 +265,7 @@ def tile_moe_nxt_lin_bias_kernel(tc, x_words, x_scales, w_words, w_scales, b, wp
 
         expert_products(0)
         group_wp(0)
+        gather_words(1, PASSES - 1)
         expert_products(1)
         quantize_wp(0)
         expert_codes(0)

@@ -9,9 +9,7 @@ PASSES = K // 512
 HALVES = N // 512
 FT = M // P
 SEQ = 48
-LOADS = 9
-ON_SCALAR = [(1, 0), (2, 0), (3, 0)]
-SCALE_RUNS = [(0, 1), (2, 3)]
+LOADS = 15
 
 FLOPS = 2 * K * N * E * C + 2 * N * M * T
 BYTES = 983040 + 30720 + 3145728 + 196608 + 16384 + 1048576 + 2048 + 8192 + 655360
@@ -48,13 +46,13 @@ def tile_moe_nxt_lin_bias_kernel(tc, x_words, x_scales, w_words, w_scales, b, wp
             nc.vector.memset(tile[:].rearrange("p a n -> p (a n)").bitcast(I32), 0)
             return tile
 
-        xs = keep.tile([P, PASSES, T], U8, name="xs", align_bytes=64)
-        nc.gpsimd.memset(xs[:].rearrange("p a t -> p (a t)").bitcast(I32), 0)
         g_rows = keep.tile([P, C], F32, name="g_rows")
-        nc.gpsimd.dma_start(g_rows[:], gate.rearrange("r (e s) -> (r e) s", s=C)[0:P])
+        nc.scalar.dma_start(g_rows[:], gate.rearrange("r (e s) -> (r e) s", s=C)[0:P])
         b_col = keep.tile([P, HALVES, 4, E], F32, name="b_col")
         nc.scalar.dma_start(b_col[:], b.rearrange("(h p j) e -> p h j e", h=HALVES, j=4))
 
+        xs = keep.tile([P, PASSES, T], U8, name="xs", align_bytes=64)
+        nc.gpsimd.memset(xs[:].rearrange("p a t -> p (a t)").bitcast(I32), 0)
         ident = keep.tile([P, P], F32, name="ident")
         make_identity(nc, ident[:])
 
@@ -62,22 +60,27 @@ def tile_moe_nxt_lin_bias_kernel(tc, x_words, x_scales, w_words, w_scales, b, wp
         nc.sync.dma_start(xw0[:], x_words[0].rearrange("p t r -> p (t r)").bitcast(I32))
         xs_rows = x_scales.rearrange("a (q r) t -> r q a t", r=4)
         for r in range(4):
-            nc.scalar.dma_start(xs[r:P:32].bitcast(I32), xs_rows[r].bitcast(I32))
-        windows = [keep.tile([P, T], F32, name="window%d" % f) for f in range(FT)]
-        nc.vector.memset(windows[0][:].bitcast(I32), 0)
-        ws = [cleared_plane([P, 2 * PASSES, N], "ws0")]
-        nc.vector.memset(windows[1][:].bitcast(I32), 0)
+            nc.sync.dma_start(xs[r:P:32].bitcast(I32), xs_rows[r].bitcast(I32))
+
+        zero = keep.tile([P, 8], F32, name="zero")
+        nc.vector.memset(zero[:], 0.0)
+        windows = [keep.tile([P, T], F32, name="window0")]
+        nc.scalar.activation(windows[0][:], zero[:, 0:1].to_broadcast([P, T]), COPY)
+
+        w_planes = [cleared_plane([P, PASSES, N], "ws%d" % e) for e in range(2)]
         xw12 = load_tile([P, 2, T], I32, "xw12")
         nc.sync.dma_start(xw12[:], x_words[1:3].rearrange("a p t r -> p a (t r)").bitcast(I32))
         x_windows = [xw0[:], xw12[:, 0, :], xw12[:, 1, :]]
+        for e in range(2, E):
+            w_planes.append(cleared_plane([P, PASSES, N], "ws%d" % e))
 
         ww = {}
         wp_raw = {}
 
-        def load_w_scales(i):
-            rows = w_scales[SCALE_RUNS[i][0] : SCALE_RUNS[i][-1] + 1].rearrange("e a (q r) n -> r q (e a) n", r=4)
+        def load_w_scales(e):
+            rows = w_scales[e].rearrange("a (q r) n -> r q a n", r=4)
             for r in range(4):
-                nc.sync.dma_start(ws[i][r:P:32].bitcast(I32), rows[r].bitcast(I32))
+                nc.sync.dma_start(w_planes[e][r:P:32].bitcast(I32), rows[r].bitcast(I32))
 
         def load_w(e):
             tile = load_tile([P, PASSES, 2 * N], U8, "ww%d" % e)
@@ -90,23 +93,24 @@ def tile_moe_nxt_lin_bias_kernel(tc, x_words, x_scales, w_words, w_scales, b, wp
             nc.sync.dma_start(tile[:].bitcast(I32), w_words[e][:, :, 1024 * h : 1024 * (h + 1)].rearrange("a p m -> p a m").bitcast(I32))
             ww[e, h] = tile[:]
 
-        def load_wp():
-            tile = load_tile([P, HALVES, 4 * M], F32, "wp_raw")
-            nc.sync.dma_start(tile[:], wp.rearrange("(h p j) f -> p h (j f)", h=HALVES, j=4))
-            for h in range(HALVES):
-                wp_raw[h] = tile[:, h, :].rearrange("p (j f) -> p j f", j=4)
+        def load_wp(h):
+            wp_raw[h] = load_tile([P, 4, M], F32, "wp_raw%d" % h)
+            nc.sync.dma_start(wp_raw[h][:], wp[512 * h : 512 * (h + 1)].rearrange("(p j) f -> p j f", j=4))
 
-        load_w(0)
-        load_w_scales(0)
-        ws.append(load_tile([P, 2 * PASSES, N], U8, "ws1"))
-        nc.vector.memset(ws[1][:].rearrange("p a n -> p (a n)").bitcast(I32), 0)
-        w_planes = {e: ws[i][:, PASSES * s : PASSES * (s + 1), :] for i, run in enumerate(SCALE_RUNS) for s, e in enumerate(run)}
-        load_w(1)
-        load_wp()
-        load_w_scales(1)
-        load_w(2)
+        for e in range(2):
+            load_w_scales(e)
         for h in range(HALVES):
-            load_w_half(3, h)
+            load_w_half(0, h)
+        load_w(1)
+        for h in range(HALVES):
+            load_wp(h)
+        for e in range(2, E):
+            load_w_scales(e)
+        windows.append(load_tile([P, T], F32, "window1"))
+        nc.vector.memset(windows[1][:].bitcast(I32), 0)
+        for e in range(2, E):
+            for h in range(HALVES):
+                load_w_half(e, h)
 
         g_col = keep.tile([P, E], F32, name="g_col")
 
@@ -142,19 +146,16 @@ def tile_moe_nxt_lin_bias_kernel(tc, x_words, x_scales, w_words, w_scales, b, wp
         def gated_bias(e):
             for h in range(HALVES):
                 gb[e, h] = keep.tile([P, 512], F32, name="gb%d_%d" % (e, h))
-                if (e, h) in ON_SCALAR:
-                    nc.scalar.activation(gb[e, h][:], spread[e, h][:].rearrange("s j p -> s (j p)"), COPY, scale=g_col[:, e : e + 1])
-                else:
-                    nc.scalar.activation(gb[e, h][:].rearrange("s (p j) -> s p j", j=4), spread[e, h][:].rearrange("s j p -> s p j"), COPY, scale=g_col[:, e : e + 1])
+                nc.scalar.activation(gb[e, h][:].rearrange("s (p j) -> s p j", j=4), spread[e, h][:].rearrange("s j p -> s p j"), COPY, scale=g_col[:, e : e + 1])
 
         wp_codes = {}
         wp_planes = {}
 
         wp_grouped = {}
 
-        def group_wp(h):
+        def group_wp(h, copy):
             wp_grouped[h] = step_tile([P, M, 4], BF16, "wp_grouped%d" % h)
-            nc.scalar.copy(wp_grouped[h][:].rearrange("p (c i) j -> p c j i", i=4), wp_raw[h].rearrange("p j (c i) -> p c j i", i=4))
+            copy(wp_grouped[h][:].rearrange("p (c i) j -> p c j i", i=4), wp_raw[h][:].rearrange("p j (c i) -> p c j i", i=4))
 
         def quantize_wp(h):
             grouped = wp_grouped[h]
@@ -185,23 +186,10 @@ def tile_moe_nxt_lin_bias_kernel(tc, x_words, x_scales, w_words, w_scales, b, wp
                 )
 
         def gate_and_bias(e, h):
-            if (e, h) in ON_SCALAR:
-                c_rows[e, h] = step_tile([P, 4, P], F32, "gated%d_%d" % (e, h))
-                nc.scalar.activation(c_rows[e, h][:], y[e, h][:].rearrange("s (p j) -> s j p", j=4), COPY, scale=g_col[:, e : e + 1])
-                return
             c_rows[e, h] = step_tile([P, 512], BF16, "c_rows%d_%d" % (e, h))
             nc.vector.scalar_tensor_tensor(c_rows[e, h][:], y[e, h][:], g_col[:, e : e + 1], gb[e, h][:], MULT, ADD)
 
         def turn(e, h):
-            if (e, h) in ON_SCALAR:
-                summed = psum.tile([P, 4, P], F32, name="summed", tag="bank")
-                for j in range(4):
-                    nc.tensor.matmul(summed[:, j, :], gb[e, h][:, P * j : P * (j + 1)], ident[:], is_transpose=True, start=(j == 0), stop=False)
-                for j in range(4):
-                    nc.tensor.matmul(summed[:, j, :], c_rows[e, h][:, j, :], ident[:], is_transpose=True, start=False, stop=(j == 3))
-                c_grouped[e, h] = step_tile([P, C, 4], BF16, "c_grouped%d_%d" % (e, h))
-                nc.scalar.copy(c_grouped[e, h][:], summed[:].rearrange("p j s -> p s j"))
-                return
             pairs = c_rows[e, h][:].bitcast(F32)
             turned = psum.tile([P, 2, P], F32, name="turned", tag="bank")
             for u in range(2):
@@ -234,12 +222,8 @@ def tile_moe_nxt_lin_bias_kernel(tc, x_words, x_scales, w_words, w_scales, b, wp
             nc.scalar.copy(o_slots[:], o[e][:, f, :])
             nc.vector.tensor_copy(windows[f][:].indirect(offsets[:, 8 * e : 8 * (e + 1)]), o_slots[:])
 
-        for e in range(2):
-            spread_bias(e)
         turn_gate()
-        for e in range(2):
-            gated_bias(e)
-        for e in range(2, E):
+        for e in range(E):
             spread_bias(e)
             gated_bias(e)
         gather_words(0, 0)
@@ -249,46 +233,45 @@ def tile_moe_nxt_lin_bias_kernel(tc, x_words, x_scales, w_words, w_scales, b, wp
             gather_words(0, a)
         for a in range(PASSES):
             gather_scales(1, a)
-        for a in range(PASSES - 1):
+        for a in range(PASSES):
             gather_words(1, a)
 
-        def expert_products(e):
-            for h in range(HALVES):
-                multiply(e, h)
-                gate_and_bias(e, h)
+        def products(e, h):
+            multiply(e, h)
+            gate_and_bias(e, h)
 
-        def expert_codes(e):
+        for e in range(2):
+            for h in range(HALVES):
+                products(e, h)
+        group_wp(0, nc.scalar.copy)
+        for e in range(2):
             for h in range(HALVES):
                 turn(e, h)
+        group_wp(1, nc.vector.tensor_copy)
+        for h in range(HALVES):
+            quantize_wp(h)
+        for e in range(2):
             for h in range(HALVES):
                 quantize_c(e, h)
-
-        expert_products(0)
-        group_wp(0)
-        gather_words(1, PASSES - 1)
-        expert_products(1)
-        quantize_wp(0)
-        expert_codes(0)
-        group_wp(1)
-
-        multiply(2, 0)
-        gate_and_bias(2, 0)
-        quantize_wp(1)
-        multiply(2, 1)
-        gate_and_bias(2, 1)
-        expert_codes(1)
-        project(0)
+            project(e)
         for f in range(FT):
             scatter(0, f)
-
-        expert_products(3)
-        expert_codes(2)
-        project(1)
         scatter(1, 0)
-        expert_codes(3)
+        products(2, 0)
         scatter(1, 1)
-        for e in range(2, E):
-            project(e)
+        products(2, 1)
+        for h in range(HALVES):
+            products(3, h)
+        for h in range(HALVES):
+            turn(2, h)
+        for h in range(HALVES):
+            quantize_c(2, h)
+        for h in range(HALVES):
+            turn(3, h)
+        project(2)
+        for h in range(HALVES):
+            quantize_c(3, h)
+        project(3)
         for e in range(2, E):
             for f in range(FT):
                 scatter(e, f)

@@ -9,7 +9,7 @@ PASSES = K // 512
 HALVES = N // 512
 FT = M // P
 SEQ = 48
-LOADS = 15
+LOADS = 20
 
 FLOPS = 2 * K * N * E * C + 2 * N * M * T
 BYTES = 983040 + 30720 + 3145728 + 196608 + 16384 + 1048576 + 2048 + 8192 + 655360
@@ -83,15 +83,9 @@ def tile_moe_nxt_lin_bias_kernel(tc, x_words, x_scales, w_words, w_scales, b, wp
                 nc.sync.dma_start(w_planes[e][r:P:32].bitcast(I32), rows[r].bitcast(I32))
 
         def load_w(e):
-            tile = load_tile([P, PASSES, 2 * N], U8, "ww%d" % e)
-            nc.sync.dma_start(tile[:].bitcast(I32), w_words[e].rearrange("a p m -> p a m").bitcast(I32))
-            for h in range(HALVES):
-                ww[e, h] = tile[:, :, 1024 * h : 1024 * (h + 1)]
-
-        def load_w_half(e, h):
-            tile = load_tile([P, PASSES, N], U8, "ww%d_%d" % (e, h))
-            nc.sync.dma_start(tile[:].bitcast(I32), w_words[e][:, :, 1024 * h : 1024 * (h + 1)].rearrange("a p m -> p a m").bitcast(I32))
-            ww[e, h] = tile[:]
+            for a in range(PASSES):
+                ww[e, a] = load_tile([P, 2 * N], U8, "ww%d_%d" % (e, a))
+                nc.sync.dma_start(ww[e, a][:].bitcast(I32), w_words[e, a].bitcast(I32))
 
         def load_wp(h):
             wp_raw[h] = load_tile([P, 4, M], F32, "wp_raw%d" % h)
@@ -99,9 +93,8 @@ def tile_moe_nxt_lin_bias_kernel(tc, x_words, x_scales, w_words, w_scales, b, wp
 
         for e in range(2):
             load_w_scales(e)
-        for h in range(HALVES):
-            load_w_half(0, h)
-        load_w(1)
+        for e in range(2):
+            load_w(e)
         for h in range(HALVES):
             load_wp(h)
         for e in range(2, E):
@@ -109,8 +102,7 @@ def tile_moe_nxt_lin_bias_kernel(tc, x_words, x_scales, w_words, w_scales, b, wp
         windows.append(load_tile([P, T], F32, "window1"))
         nc.vector.memset(windows[1][:].bitcast(I32), 0)
         for e in range(2, E):
-            for h in range(HALVES):
-                load_w_half(e, h)
+            load_w(e)
 
         g_col = keep.tile([P, E], F32, name="g_col")
 
@@ -170,20 +162,22 @@ def tile_moe_nxt_lin_bias_kernel(tc, x_words, x_scales, w_words, w_scales, b, wp
         c_planes = {}
         o = {}
 
-        def multiply(e, h):
+        def multiply(e):
             i, s = divmod(e, 2)
             slots = slice(s * C, (s + 1) * C)
-            y[e, h] = psum.tile([P, 512], F32, name="y", tag="bank")
             for a in range(PASSES):
-                nc.tensor.matmul_mx(
-                    out=y[e, h][:],
-                    lhsT=gw[i, a][:, slots].bitcast(FP8X4),
-                    lhsT_scale=gs[i, a][:, slots],
-                    rhs=ww[e, h][:, a, :].bitcast(FP4X4),
-                    rhs_scale=w_planes[e][:, a, 512 * h : 512 * (h + 1)],
-                    start=(a == 0),
-                    stop=(a == PASSES - 1),
-                )
+                for h in range(HALVES):
+                    if a == 0:
+                        y[e, h] = psum.tile([P, 512], F32, name="y", tag="bank")
+                    nc.tensor.matmul_mx(
+                        out=y[e, h][:],
+                        lhsT=gw[i, a][:, slots].bitcast(FP8X4),
+                        lhsT_scale=gs[i, a][:, slots],
+                        rhs=ww[e, a][:, N * h : N * (h + 1)].bitcast(FP4X4),
+                        rhs_scale=w_planes[e][:, a, 512 * h : 512 * (h + 1)],
+                        start=(a == 0),
+                        stop=(a == PASSES - 1),
+                    )
 
         def gate_and_bias(e, h):
             c_rows[e, h] = step_tile([P, 512], BF16, "c_rows%d_%d" % (e, h))
@@ -237,7 +231,8 @@ def tile_moe_nxt_lin_bias_kernel(tc, x_words, x_scales, w_words, w_scales, b, wp
             gather_words(1, a)
 
         def products(e, h):
-            multiply(e, h)
+            if h == 0:
+                multiply(e)
             gate_and_bias(e, h)
 
         for e in range(2):

@@ -39,7 +39,7 @@ def tile_moe_nxt_lin_bias_kernel(tc, x_words, x_scales, w_words, w_scales, b, wp
         nc.sync.dma_start(offsets[:], offs)
 
         def load_tile(shape, dtype, name):
-            return loads.tile(shape, dtype, name=name, tag="load", align_bytes=64)
+            return loads.tile(shape, dtype, name=name, tag="load", align_bytes=256)
 
         def cleared_plane(shape, name):
             tile = load_tile(shape, U8, name)

@@ -33,89 +33,124 @@ def tile_moe_nxt_lin_bias_kernel(tc, x_words, x_scales, w_words, w_scales, b, wp
         keep = ctx.enter_context(tc.tile_pool(name="keep", bufs=1))
         steps = ctx.enter_context(tc.tile_pool(name="steps", bufs=SEQ))
         psum = ctx.enter_context(tc.psum_pool(name="psum", bufs=8))
-
         loads = ctx.enter_context(tc.tile_pool(name="loads", bufs=LOADS))
+
         offsets = keep.tile([P, E * C // 16], U16, name="offsets")
         nc.sync.dma_start(offsets[:], offs)
+
+        def keep_tile(shape, dtype, name):
+            return keep.tile(shape, dtype, name=name, align_bytes=64)
 
         def load_tile(shape, dtype, name):
             return loads.tile(shape, dtype, name=name, tag="load", align_bytes=256)
 
-        def cleared_plane(shape, name):
-            tile = load_tile(shape, U8, name)
-            nc.vector.memset(tile[:].rearrange("p a n -> p (a n)").bitcast(I32), 0)
-            return tile
+        def step_tile(shape, dtype, name):
+            return steps.tile(shape, dtype, name=name, tag="step", align_bytes=64)
 
-        g_rows = keep.tile([P, C], F32, name="g_rows")
-        nc.scalar.dma_start(g_rows[:], gate.rearrange("r (e s) -> (r e) s", s=C)[0:P])
-        b_col = keep.tile([P, HALVES, 4, E], F32, name="b_col")
-        nc.scalar.dma_start(b_col[:], b.rearrange("(h p j) e -> p h j e", h=HALVES, j=4))
+        def bank(shape, name):
+            return psum.tile(shape, F32, name=name, tag="bank")
 
-        xs = keep.tile([P, PASSES, T], U8, name="xs", align_bytes=64)
-        nc.gpsimd.memset(xs[:].rearrange("p a t -> p (a t)").bitcast(I32), 0)
-        ident = keep.tile([P, P], F32, name="ident")
-        make_identity(nc, ident[:])
-
-        xw0 = keep.tile([P, T], I32, name="xw0")
-        nc.sync.dma_start(xw0[:], x_words[0].rearrange("p t r -> p (t r)").bitcast(I32))
-        xs_rows = x_scales.rearrange("a (q r) t -> r q a t", r=4)
-        for r in range(4):
-            nc.sync.dma_start(xs[r:P:32].bitcast(I32), xs_rows[r].bitcast(I32))
-
-        zero = keep.tile([P, 8], F32, name="zero")
-        nc.vector.memset(zero[:], 0.0)
-        windows = [keep.tile([P, T], F32, name="window0")]
-        nc.scalar.activation(windows[0][:], zero[:, 0:1].to_broadcast([P, T]), COPY)
-
-        w_planes = [cleared_plane([P, PASSES, N], "ws%d" % e) for e in range(2)]
-        xw12 = load_tile([P, 2, T], I32, "xw12")
-        nc.sync.dma_start(xw12[:], x_words[1:3].rearrange("a p t r -> p a (t r)").bitcast(I32))
-        x_windows = [xw0[:], xw12[:, 0, :], xw12[:, 1, :]]
-        for e in range(2, E):
-            w_planes.append(cleared_plane([P, PASSES, N], "ws%d" % e))
-
+        x_windows = {}
         ww = {}
         wp_raw = {}
+        w_planes = {}
+        windows = {}
+
+        def load_x(first, last, make_tile):
+            tile = make_tile([P, last - first, T], I32, "xw%d" % first)
+            nc.sync.dma_start(tile[:], x_words[first:last].rearrange("a p t r -> p a (t r)").bitcast(I32))
+            for a in range(first, last):
+                x_windows[a] = tile[:, a - first, :]
+
+        def clear_plane(e):
+            w_planes[e] = load_tile([P, PASSES, N], U8, "ws%d" % e)
+            nc.vector.memset(w_planes[e][:].rearrange("p a n -> p (a n)").bitcast(I32), 0)
 
         def load_w_scales(e):
             rows = w_scales[e].rearrange("a (q r) n -> r q a n", r=4)
             for r in range(4):
                 nc.sync.dma_start(w_planes[e][r:P:32].bitcast(I32), rows[r].bitcast(I32))
 
-        def load_w(e):
-            for a in range(PASSES):
-                ww[e, a] = load_tile([P, 2 * N], U8, "ww%d_%d" % (e, a))
-                nc.sync.dma_start(ww[e, a][:].bitcast(I32), w_words[e, a].bitcast(I32))
+        def load_w(e, a, make_tile=load_tile):
+            tile = make_tile([P, 2 * N], U8, "ww%d_%d" % (e, a))
+            nc.sync.dma_start(tile[:].bitcast(I32), w_words[e, a].bitcast(I32))
+            for h in range(HALVES):
+                ww[e, a, h] = tile[:, N * h : N * (h + 1)]
+
+        def load_w_half(e, h, first, last, make_tile=load_tile):
+            tile = make_tile([P, last - first, N], U8, "ww%d_%d_%d" % (e, h, first))
+            nc.sync.dma_start(tile[:].bitcast(I32), w_words[e, first:last][:, :, N * h : N * (h + 1)].rearrange("a p m -> p a m").bitcast(I32))
+            for a in range(first, last):
+                ww[e, a, h] = tile[:, a - first, :]
 
         def load_wp(h):
             wp_raw[h] = load_tile([P, 4, M], F32, "wp_raw%d" % h)
             nc.sync.dma_start(wp_raw[h][:], wp[512 * h : 512 * (h + 1)].rearrange("(p j) f -> p j f", j=4))
 
+        g_rows = keep.tile([P, C], F32, name="g_rows")
+        nc.scalar.dma_start(g_rows[:], gate.rearrange("r (e s) -> (r e) s", s=C)[0:P])
+        b_col = keep.tile([P, HALVES, 4, E], F32, name="b_col")
+        nc.scalar.dma_start(b_col[:], b.rearrange("(h p j) e -> p h j e", h=HALVES, j=4))
+
+        xs = keep_tile([P, PASSES, T], U8, "xs")
+        nc.gpsimd.memset(xs[:].rearrange("p a t -> p (a t)").bitcast(I32), 0)
+        ident = keep.tile([P, P], F32, name="ident")
+        make_identity(nc, ident[:])
+
+        load_x(0, 1, keep_tile)
+        xs_rows = x_scales.rearrange("a (q r) t -> r q a t", r=4)
+        for r in range(4):
+            nc.sync.dma_start(xs[r:P:32].bitcast(I32), xs_rows[r].bitcast(I32))
+
+        zero = keep.tile([P, 8], F32, name="zero")
+        nc.vector.memset(zero[:], 0.0)
+        windows[0] = keep.tile([P, T], F32, name="window0")
+        nc.scalar.activation(windows[0][:], zero[:, 0:1].to_broadcast([P, T]), COPY)
+
         for e in range(2):
-            load_w_scales(e)
-        for e in range(2):
-            load_w(e)
-        for h in range(HALVES):
-            load_wp(h)
+            clear_plane(e)
+        load_x(1, 3, load_tile)
         for e in range(2, E):
-            load_w_scales(e)
-        windows.append(load_tile([P, T], F32, "window1"))
+            clear_plane(e)
+        load_w_scales(0)
+        load_w_scales(1)
+        for a in range(PASSES):
+            load_w(0, a)
+        for a in range(PASSES):
+            load_w(1, a)
+        load_wp(0)
+        load_wp(1)
+        load_w_scales(2)
+        load_w_scales(3)
+        windows[1] = load_tile([P, T], F32, "window1")
         nc.vector.memset(windows[1][:].bitcast(I32), 0)
-        for e in range(2, E):
-            load_w(e)
+        load_w(2, 0)
+        load_w(2, 1)
+        load_w(3, 0)
+        load_w(2, 2)
+        load_w(3, 1)
+        load_w(3, 2)
 
         g_col = keep.tile([P, E], F32, name="g_col")
-
-        def turn_gate():
-            g_turned = psum.tile([P, C], F32, name="g_turned", tag="bank")
-            nc.tensor.transpose(g_turned[:], g_rows[:], ident[:])
-            nc.scalar.copy(g_col[:], g_turned[:, 0:E])
-
-        def step_tile(shape, dtype, name):
-            return steps.tile(shape, dtype, name=name, tag="step", align_bytes=64)
-
         gw = {}
         gs = {}
+        gb = {}
+        spread = {}
+        wp_grouped = {}
+        wp_codes = {}
+        wp_planes = {}
+        y = {}
+        c_rows = {}
+        c_grouped = {}
+        c_codes = {}
+        c_planes = {}
+        o = {}
+        o_slots = {}
+
+        def turn_gate():
+            g_turned = bank([P, C], "g_turned")
+            nc.tensor.transpose(g_turned[:], g_rows[:], ident[:])
+            nc.scalar.copy(g_col[:], g_turned[:, 0:E])
 
         def gather_scales(i, a):
             gs[i, a] = step_tile([P, 2 * C], U8, "gs%d_%d" % (i, a))
@@ -125,13 +160,9 @@ def tile_moe_nxt_lin_bias_kernel(tc, x_words, x_scales, w_words, w_scales, b, wp
             gw[i, a] = step_tile([P, 2 * C], U32, "gw%d_%d" % (i, a))
             nc.vector.tensor_copy(gw[i, a][:], x_windows[a].bitcast(U32).indirect(offsets[:, 16 * i : 16 * (i + 1)]))
 
-        gb = {}
-
-        spread = {}
-
         def spread_bias(e):
             for h in range(HALVES):
-                spread[e, h] = psum.tile([P, 4, P], F32, name="spread", tag="bank")
+                spread[e, h] = bank([P, 4, P], "spread")
                 for j in range(4):
                     nc.tensor.transpose(spread[e, h][:, j, :], b_col[:, h, j, e : e + 1].to_broadcast([P, P]), ident[:])
 
@@ -140,52 +171,47 @@ def tile_moe_nxt_lin_bias_kernel(tc, x_words, x_scales, w_words, w_scales, b, wp
                 gb[e, h] = keep.tile([P, 512], F32, name="gb%d_%d" % (e, h))
                 nc.scalar.activation(gb[e, h][:].rearrange("s (p j) -> s p j", j=4), spread[e, h][:].rearrange("s j p -> s p j"), COPY, scale=g_col[:, e : e + 1])
 
-        wp_codes = {}
-        wp_planes = {}
-
-        wp_grouped = {}
-
         def group_wp(h, copy):
             wp_grouped[h] = step_tile([P, M, 4], BF16, "wp_grouped%d" % h)
             copy(wp_grouped[h][:].rearrange("p (c i) j -> p c j i", i=4), wp_raw[h][:].rearrange("p j (c i) -> p c j i", i=4))
 
         def quantize_wp(h):
-            grouped = wp_grouped[h]
             wp_codes[h] = step_tile([P, M], U32, "wp_codes%d" % h)
-            wp_planes[h] = keep.tile([P, M], U8, name="wp_planes%d" % h, align_bytes=64)
-            nc.vector.quantize_mx(out=wp_codes[h][:].bitcast(FP8X4), scales=wp_planes[h][:], in_=grouped[:].rearrange("p f j -> p (f j)"))
+            wp_planes[h] = keep_tile([P, M], U8, "wp_planes%d" % h)
+            nc.vector.quantize_mx(out=wp_codes[h][:].bitcast(FP8X4), scales=wp_planes[h][:], in_=wp_grouped[h][:].rearrange("p f j -> p (f j)"))
 
-        y = {}
-        c_rows = {}
-        c_grouped = {}
-        c_codes = {}
-        c_planes = {}
-        o = {}
-
-        def multiply(e):
+        def multiply(e, a, h, order=(0, 1, 2)):
             i, s = divmod(e, 2)
             slots = slice(s * C, (s + 1) * C)
-            for a in range(PASSES):
-                for h in range(HALVES):
-                    if a == 0:
-                        y[e, h] = psum.tile([P, 512], F32, name="y", tag="bank")
-                    nc.tensor.matmul_mx(
-                        out=y[e, h][:],
-                        lhsT=gw[i, a][:, slots].bitcast(FP8X4),
-                        lhsT_scale=gs[i, a][:, slots],
-                        rhs=ww[e, a][:, N * h : N * (h + 1)].bitcast(FP4X4),
-                        rhs_scale=w_planes[e][:, a, 512 * h : 512 * (h + 1)],
-                        start=(a == 0),
-                        stop=(a == PASSES - 1),
-                    )
+            if a == order[0]:
+                y[e, h] = bank([P, 512], "y")
+            nc.tensor.matmul_mx(
+                out=y[e, h][:],
+                lhsT=gw[i, a][:, slots].bitcast(FP8X4),
+                lhsT_scale=gs[i, a][:, slots],
+                rhs=ww[e, a, h].bitcast(FP4X4),
+                rhs_scale=w_planes[e][:, a, 512 * h : 512 * (h + 1)],
+                start=(a == order[0]),
+                stop=(a == order[-1]),
+            )
 
-        def gate_and_bias(e, h):
-            c_rows[e, h] = step_tile([P, 512], BF16, "c_rows%d_%d" % (e, h))
+        def multiply_by_pass(e, first=0, last=PASSES):
+            for a in range(first, last):
+                for h in range(HALVES):
+                    multiply(e, a, h)
+
+        def multiply_half(e, h):
+            order = (0, 1, 2) if h == 0 else (2, 0, 1)
+            for a in order:
+                multiply(e, a, h, order)
+
+        def gate_and_bias(e, h, make_tile=step_tile):
+            c_rows[e, h] = make_tile([P, 512], BF16, "c_rows%d_%d" % (e, h))
             nc.vector.scalar_tensor_tensor(c_rows[e, h][:], y[e, h][:], g_col[:, e : e + 1], gb[e, h][:], MULT, ADD)
 
         def turn(e, h):
             pairs = c_rows[e, h][:].bitcast(F32)
-            turned = psum.tile([P, 2, P], F32, name="turned", tag="bank")
+            turned = bank([P, 2, P], "turned")
             for u in range(2):
                 nc.tensor.transpose(turned[:, u, :], pairs[:, u:256:2], ident[:])
             c_grouped[e, h] = step_tile([P, C, 4], BF16, "c_grouped%d_%d" % (e, h))
@@ -193,83 +219,117 @@ def tile_moe_nxt_lin_bias_kernel(tc, x_words, x_scales, w_words, w_scales, b, wp
 
         def quantize_c(e, h):
             c_codes[e, h] = step_tile([P, C], U32, "c_codes%d_%d" % (e, h))
-            c_planes[e, h] = keep.tile([P, C], U8, name="c_planes%d_%d" % (e, h), align_bytes=64)
+            c_planes[e, h] = keep_tile([P, C], U8, "c_planes%d_%d" % (e, h))
             nc.vector.quantize_mx(out=c_codes[e, h][:].bitcast(FP8X4), scales=c_planes[e, h][:], in_=c_grouped[e, h][:].rearrange("p s j -> p (s j)"))
 
+        def project_pass(e, f, h, start, stop):
+            cols = slice(f * P, (f + 1) * P)
+            nc.tensor.matmul_mx(
+                out=o[e][:, f, :],
+                lhsT=wp_codes[h][:, cols].bitcast(FP8X4),
+                lhsT_scale=wp_planes[h][:, cols],
+                rhs=c_codes[e, h][:].bitcast(FP8X4),
+                rhs_scale=c_planes[e, h][:],
+                start=start,
+                stop=stop,
+            )
+
         def project(e):
-            o[e] = psum.tile([P, FT, C], F32, name="o", tag="bank")
+            o[e] = bank([P, FT, C], "o")
             for f in range(FT):
-                cols = slice(f * P, (f + 1) * P)
                 for h in range(HALVES):
-                    nc.tensor.matmul_mx(
-                        out=o[e][:, f, :],
-                        lhsT=wp_codes[h][:, cols].bitcast(FP8X4),
-                        lhsT_scale=wp_planes[h][:, cols],
-                        rhs=c_codes[e, h][:].bitcast(FP8X4),
-                        rhs_scale=c_planes[e, h][:],
-                        start=(h == 0),
-                        stop=(h == HALVES - 1),
-                    )
+                    project_pass(e, f, h, h == 0, h == HALVES - 1)
+
+        def project_half(e, h):
+            if h == 0:
+                o[e] = bank([P, FT, C], "o")
+            for f in range(FT):
+                project_pass(e, f, h, h == 0 and f == 0, h == HALVES - 1 and f == FT - 1)
+
+        def leave_bank(e, f):
+            o_slots[e, f] = step_tile([P, C], F32, "o_slots%d_%d" % (e, f))
+            nc.scalar.copy(o_slots[e, f][:], o[e][:, f, :])
 
         def scatter(e, f):
-            o_slots = step_tile([P, C], F32, "o_slots%d_%d" % (e, f))
-            nc.scalar.copy(o_slots[:], o[e][:, f, :])
-            nc.vector.tensor_copy(windows[f][:].indirect(offsets[:, 8 * e : 8 * (e + 1)]), o_slots[:])
+            nc.vector.tensor_copy(windows[f][:].indirect(offsets[:, 8 * e : 8 * (e + 1)]), o_slots[e, f][:])
 
         turn_gate()
-        for e in range(E):
-            spread_bias(e)
-            gated_bias(e)
+        spread_bias(0)
+        gated_bias(0)
+        spread_bias(1)
+        gated_bias(1)
+        spread_bias(2)
+        gated_bias(2)
+        spread_bias(3)
+        gated_bias(3)
         gather_words(0, 0)
-        for a in range(PASSES):
-            gather_scales(0, a)
-        for a in range(1, PASSES):
-            gather_words(0, a)
-        for a in range(PASSES):
-            gather_scales(1, a)
-        for a in range(PASSES):
-            gather_words(1, a)
-
-        def products(e, h):
-            if h == 0:
-                multiply(e)
-            gate_and_bias(e, h)
-
-        for e in range(2):
-            for h in range(HALVES):
-                products(e, h)
+        gather_scales(0, 0)
+        gather_scales(0, 1)
+        gather_scales(0, 2)
+        gather_words(0, 1)
+        gather_words(0, 2)
+        gather_scales(1, 0)
+        gather_scales(1, 1)
+        gather_scales(1, 2)
+        gather_words(1, 0)
+        gather_words(1, 1)
+        gather_words(1, 2)
+        multiply_by_pass(0)
+        gate_and_bias(0, 0)
+        gate_and_bias(0, 1)
+        multiply_by_pass(1)
+        gate_and_bias(1, 0)
+        gate_and_bias(1, 1)
         group_wp(0, nc.scalar.copy)
-        for e in range(2):
-            for h in range(HALVES):
-                turn(e, h)
+        turn(0, 0)
+        turn(0, 1)
+        turn(1, 0)
+        turn(1, 1)
         group_wp(1, nc.vector.tensor_copy)
-        for h in range(HALVES):
-            quantize_wp(h)
-        for e in range(2):
-            for h in range(HALVES):
-                quantize_c(e, h)
-            project(e)
-        for f in range(FT):
-            scatter(0, f)
+        quantize_wp(0)
+        quantize_wp(1)
+        quantize_c(0, 0)
+        quantize_c(0, 1)
+        project(0)
+        quantize_c(1, 0)
+        quantize_c(1, 1)
+        project(1)
+        leave_bank(0, 0)
+        scatter(0, 0)
+        leave_bank(0, 1)
+        scatter(0, 1)
+        leave_bank(1, 0)
         scatter(1, 0)
-        products(2, 0)
-        scatter(1, 1)
-        products(2, 1)
-        for h in range(HALVES):
-            products(3, h)
-        for h in range(HALVES):
-            turn(2, h)
-        for h in range(HALVES):
-            quantize_c(2, h)
-        for h in range(HALVES):
-            turn(3, h)
+        multiply_by_pass(2, 0, 1)
+        multiply_by_pass(2, 1, 2)
+        multiply_by_pass(3, 0, 1)
+        multiply_by_pass(2, 2, 3)
+        gate_and_bias(2, 0)
+        gate_and_bias(2, 1)
+        multiply_by_pass(3, 1, 2)
+        multiply_by_pass(3, 2, 3)
+        gate_and_bias(3, 0)
+        gate_and_bias(3, 1)
+        turn(2, 0)
+        turn(2, 1)
+        quantize_c(2, 0)
+        leave_bank(1, 1)
+        quantize_c(2, 1)
+        turn(3, 0)
+        turn(3, 1)
         project(2)
-        for h in range(HALVES):
-            quantize_c(3, h)
+        scatter(1, 1)
+        quantize_c(3, 0)
+        leave_bank(2, 0)
+        leave_bank(2, 1)
+        quantize_c(3, 1)
         project(3)
-        for e in range(2, E):
-            for f in range(FT):
-                scatter(e, f)
+        scatter(2, 0)
+        scatter(2, 1)
+        leave_bank(3, 0)
+        leave_bank(3, 1)
+        scatter(3, 0)
+        scatter(3, 1)
 
         nc.sync.dma_start(out[0:P, :], windows[0][:])
         nc.scalar.dma_start(out[P : 2 * P, :], windows[1][:])

@@ -8,8 +8,6 @@ P = 128
 PASSES = K // 512
 HALVES = N // 512
 FT = M // P
-SEQ = 48
-LOADS = 20
 
 FLOPS = 2 * K * N * E * C + 2 * N * M * T
 BYTES = 983040 + 30720 + 3145728 + 196608 + 16384 + 1048576 + 2048 + 8192 + 655360
@@ -31,9 +29,10 @@ def tile_moe_nxt_lin_bias_kernel(tc, x_words, x_scales, w_words, w_scales, b, wp
     nc = tc.nc
     with ExitStack() as ctx:
         keep = ctx.enter_context(tc.tile_pool(name="keep", bufs=1))
-        steps = ctx.enter_context(tc.tile_pool(name="steps", bufs=SEQ))
+        loads = ctx.enter_context(tc.tile_pool(name="loads", bufs=22))
+        vec = ctx.enter_context(tc.tile_pool(name="vec", bufs=32))
+        act = ctx.enter_context(tc.tile_pool(name="act", bufs=30))
         psum = ctx.enter_context(tc.psum_pool(name="psum", bufs=8))
-        loads = ctx.enter_context(tc.tile_pool(name="loads", bufs=LOADS))
 
         offsets = keep.tile([P, E * C // 16], U16, name="offsets")
         nc.sync.dma_start(offsets[:], offs)
@@ -44,8 +43,11 @@ def tile_moe_nxt_lin_bias_kernel(tc, x_words, x_scales, w_words, w_scales, b, wp
         def load_tile(shape, dtype, name):
             return loads.tile(shape, dtype, name=name, tag="load", align_bytes=256)
 
-        def step_tile(shape, dtype, name):
-            return steps.tile(shape, dtype, name=name, tag="step", align_bytes=64)
+        def vec_tile(shape, dtype, name):
+            return vec.tile(shape, dtype, name=name, tag="vec", align_bytes=64)
+
+        def act_tile(shape, dtype, name):
+            return act.tile(shape, dtype, name=name, tag="act", align_bytes=64)
 
         def bank(shape, name):
             return psum.tile(shape, F32, name=name, tag="bank")
@@ -55,83 +57,6 @@ def tile_moe_nxt_lin_bias_kernel(tc, x_words, x_scales, w_words, w_scales, b, wp
         wp_raw = {}
         w_planes = {}
         windows = {}
-
-        def load_x(first, last, make_tile):
-            tile = make_tile([P, last - first, T], I32, "xw%d" % first)
-            nc.sync.dma_start(tile[:], x_words[first:last].rearrange("a p t r -> p a (t r)").bitcast(I32))
-            for a in range(first, last):
-                x_windows[a] = tile[:, a - first, :]
-
-        def clear_plane(e):
-            w_planes[e] = load_tile([P, PASSES, N], U8, "ws%d" % e)
-            nc.vector.memset(w_planes[e][:].rearrange("p a n -> p (a n)").bitcast(I32), 0)
-
-        def load_w_scales(e):
-            rows = w_scales[e].rearrange("a (q r) n -> r q a n", r=4)
-            for r in range(4):
-                nc.sync.dma_start(w_planes[e][r:P:32].bitcast(I32), rows[r].bitcast(I32))
-
-        def load_w(e, a, make_tile=load_tile):
-            tile = make_tile([P, 2 * N], U8, "ww%d_%d" % (e, a))
-            nc.sync.dma_start(tile[:].bitcast(I32), w_words[e, a].bitcast(I32))
-            for h in range(HALVES):
-                ww[e, a, h] = tile[:, N * h : N * (h + 1)]
-
-        def load_w_half(e, h, first, last, make_tile=load_tile):
-            tile = make_tile([P, last - first, N], U8, "ww%d_%d_%d" % (e, h, first))
-            nc.sync.dma_start(tile[:].bitcast(I32), w_words[e, first:last][:, :, N * h : N * (h + 1)].rearrange("a p m -> p a m").bitcast(I32))
-            for a in range(first, last):
-                ww[e, a, h] = tile[:, a - first, :]
-
-        def load_wp(h):
-            wp_raw[h] = load_tile([P, 4, M], F32, "wp_raw%d" % h)
-            nc.sync.dma_start(wp_raw[h][:], wp[512 * h : 512 * (h + 1)].rearrange("(p j) f -> p j f", j=4))
-
-        g_rows = keep.tile([P, C], F32, name="g_rows")
-        nc.scalar.dma_start(g_rows[:], gate.rearrange("r (e s) -> (r e) s", s=C)[0:P])
-        b_col = keep.tile([P, HALVES, 4, E], F32, name="b_col")
-        nc.scalar.dma_start(b_col[:], b.rearrange("(h p j) e -> p h j e", h=HALVES, j=4))
-
-        xs = keep_tile([P, PASSES, T], U8, "xs")
-        nc.gpsimd.memset(xs[:].rearrange("p a t -> p (a t)").bitcast(I32), 0)
-        ident = keep.tile([P, P], F32, name="ident")
-        make_identity(nc, ident[:])
-
-        load_x(0, 1, keep_tile)
-        xs_rows = x_scales.rearrange("a (q r) t -> r q a t", r=4)
-        for r in range(4):
-            nc.sync.dma_start(xs[r:P:32].bitcast(I32), xs_rows[r].bitcast(I32))
-
-        zero = keep.tile([P, 8], F32, name="zero")
-        nc.vector.memset(zero[:], 0.0)
-        windows[0] = keep.tile([P, T], F32, name="window0")
-        nc.scalar.activation(windows[0][:], zero[:, 0:1].to_broadcast([P, T]), COPY)
-
-        for e in range(2):
-            clear_plane(e)
-        load_x(1, 3, load_tile)
-        for e in range(2, E):
-            clear_plane(e)
-        load_w_scales(0)
-        load_w_scales(1)
-        for a in range(PASSES):
-            load_w(0, a)
-        for a in range(PASSES):
-            load_w(1, a)
-        load_wp(0)
-        load_wp(1)
-        load_w_scales(2)
-        load_w_scales(3)
-        windows[1] = load_tile([P, T], F32, "window1")
-        nc.vector.memset(windows[1][:].bitcast(I32), 0)
-        load_w(2, 0)
-        load_w(2, 1)
-        load_w(3, 0)
-        load_w(2, 2)
-        load_w(3, 1)
-        load_w(3, 2)
-
-        g_col = keep.tile([P, E], F32, name="g_col")
         gw = {}
         gs = {}
         gb = {}
@@ -141,91 +66,138 @@ def tile_moe_nxt_lin_bias_kernel(tc, x_words, x_scales, w_words, w_scales, b, wp
         wp_planes = {}
         y = {}
         c_rows = {}
+        turned = {}
         c_grouped = {}
         c_codes = {}
         c_planes = {}
         o = {}
         o_slots = {}
+        small = {}
+
+        def cleared_plane(width, name, memset):
+            plane = load_tile([P, PASSES, width], U8, name)
+            memset(plane[:].rearrange("p a n -> p (a n)").bitcast(I32), 0)
+            return plane
+
+        def load_scale_rows(plane, scales):
+            rows = scales.rearrange("a (q r) n -> r q a n", r=4)
+            for r in range(4):
+                nc.sync.dma_start(plane[r:P:32].bitcast(I32), rows[r].bitcast(I32))
+
+        def load_x(first, last):
+            tile = keep.tile([P, last - first, T], I32, name="xw%d" % first, align_bytes=256)
+            nc.sync.dma_start(tile[:], x_words[first:last].rearrange("a p t r -> p a (t r)").bitcast(I32))
+            for a in range(first, last):
+                x_windows[a] = tile[:, a - first, :]
+
+        def load_w(e, a):
+            ww[e, a] = load_tile([P, 2 * N], U8, "ww%d_%d" % (e, a))
+            nc.sync.dma_start(ww[e, a][:].bitcast(I32), w_words[e, a].bitcast(I32))
+
+        def load_expert(e):
+            for a in range(PASSES):
+                load_w(e, a)
+
+        def load_wp(h):
+            wp_raw[h] = load_tile([P, 4, M], F32, "wp_raw%d" % h)
+            nc.sync.dma_start(wp_raw[h][:], wp[512 * h : 512 * (h + 1)].rearrange("(p j) f -> p j f", j=4))
+
+        def load_bias():
+            small["b"] = keep.tile([P, HALVES, 4, E], F32, name="b_col")
+            nc.scalar.dma_start(small["b"][:], b.rearrange("(h p j) e -> p h j e", h=HALVES, j=4))
+
+        def load_gate(make_tile):
+            small["g_rows"] = make_tile([P, C], F32, "g_rows")
+            nc.scalar.dma_start(small["g_rows"][:], gate.rearrange("r (e s) -> (r e) s", s=C)[0:P])
+
+        def clear_window(f):
+            windows[f] = keep.tile([P, T], F32, name="window%d" % f)
+            nc.scalar.activation(windows[f][:], small["zero"][:, 0:1].to_broadcast([P, T]), COPY)
 
         def turn_gate():
             g_turned = bank([P, C], "g_turned")
-            nc.tensor.transpose(g_turned[:], g_rows[:], ident[:])
-            nc.scalar.copy(g_col[:], g_turned[:, 0:E])
+            nc.tensor.transpose(g_turned[:], small["g_rows"][:], ident[:])
+            small["g"] = act_tile([P, E], F32, "g_col")
+            nc.scalar.copy(small["g"][:], g_turned[:, 0:E])
 
         def gather_scales(i, a):
-            gs[i, a] = step_tile([P, 2 * C], U8, "gs%d_%d" % (i, a))
+            gs[i, a] = vec_tile([P, 2 * C], U8, "gs%d_%d" % (i, a))
             nc.vector.tensor_copy(gs[i, a][:], xs[:, a, :].indirect(offsets[:, 16 * i : 16 * (i + 1)]))
 
-        def gather_words(i, a):
-            gw[i, a] = step_tile([P, 2 * C], U32, "gw%d_%d" % (i, a))
+        def gather_words(i, a, make_tile=vec_tile):
+            gw[i, a] = make_tile([P, 2 * C], U32, "gw%d_%d" % (i, a))
             nc.vector.tensor_copy(gw[i, a][:], x_windows[a].bitcast(U32).indirect(offsets[:, 16 * i : 16 * (i + 1)]))
 
         def spread_bias(e):
             for h in range(HALVES):
                 spread[e, h] = bank([P, 4, P], "spread")
                 for j in range(4):
-                    nc.tensor.transpose(spread[e, h][:, j, :], b_col[:, h, j, e : e + 1].to_broadcast([P, P]), ident[:])
+                    nc.tensor.transpose(spread[e, h][:, j, :], small["b"][:, h, j, e : e + 1].to_broadcast([P, P]), ident[:])
 
         def gated_bias(e):
             for h in range(HALVES):
-                gb[e, h] = keep.tile([P, 512], F32, name="gb%d_%d" % (e, h))
-                nc.scalar.activation(gb[e, h][:].rearrange("s (p j) -> s p j", j=4), spread[e, h][:].rearrange("s j p -> s p j"), COPY, scale=g_col[:, e : e + 1])
+                gb[e, h] = act_tile([P, 512], F32, "gb%d_%d" % (e, h))
+                nc.scalar.activation(gb[e, h][:].rearrange("s (u p i) -> s u p i", u=2, i=2), spread[e, h][:].rearrange("s (u i) p -> s u p i", u=2), COPY, scale=small["g"][:, e : e + 1])
 
-        def group_wp(h, copy):
-            wp_grouped[h] = step_tile([P, M, 4], BF16, "wp_grouped%d" % h)
+        def group_wp(h, copy, make_tile):
+            wp_grouped[h] = make_tile([P, M, 4], BF16, "wp_grouped%d" % h)
             copy(wp_grouped[h][:].rearrange("p (c i) j -> p c j i", i=4), wp_raw[h][:].rearrange("p j (c i) -> p c j i", i=4))
 
         def quantize_wp(h):
-            wp_codes[h] = step_tile([P, M], U32, "wp_codes%d" % h)
+            wp_codes[h] = vec_tile([P, M], U32, "wp_codes%d" % h)
             wp_planes[h] = keep_tile([P, M], U8, "wp_planes%d" % h)
             nc.vector.quantize_mx(out=wp_codes[h][:].bitcast(FP8X4), scales=wp_planes[h][:], in_=wp_grouped[h][:].rearrange("p f j -> p (f j)"))
 
-        def multiply(e, a, h, order=(0, 1, 2)):
+        def multiply(e, a, h, start, stop):
             i, s = divmod(e, 2)
             slots = slice(s * C, (s + 1) * C)
-            if a == order[0]:
-                y[e, h] = bank([P, 512], "y")
             nc.tensor.matmul_mx(
                 out=y[e, h][:],
                 lhsT=gw[i, a][:, slots].bitcast(FP8X4),
                 lhsT_scale=gs[i, a][:, slots],
-                rhs=ww[e, a, h].bitcast(FP4X4),
+                rhs=ww[e, a][:, N * h : N * (h + 1)].bitcast(FP4X4),
                 rhs_scale=w_planes[e][:, a, 512 * h : 512 * (h + 1)],
-                start=(a == order[0]),
-                stop=(a == order[-1]),
+                start=start,
+                stop=stop,
             )
 
-        def multiply_by_pass(e, first=0, last=PASSES):
-            for a in range(first, last):
-                for h in range(HALVES):
-                    multiply(e, a, h)
+        def first_pass(e):
+            for h in range(HALVES):
+                y[e, h] = bank([P, 512], "y")
+                multiply(e, 0, h, True, False)
 
-        def multiply_half(e, h):
-            order = (0, 1, 2) if h == 0 else (2, 0, 1)
-            for a in order:
-                multiply(e, a, h, order)
+        def later_passes(e):
+            multiply(e, 1, 0, False, False)
+            multiply(e, 2, 0, False, True)
+            multiply(e, 2, 1, False, False)
+            multiply(e, 1, 1, False, True)
 
-        def gate_and_bias(e, h, make_tile=step_tile):
-            c_rows[e, h] = make_tile([P, 512], BF16, "c_rows%d_%d" % (e, h))
-            nc.vector.scalar_tensor_tensor(c_rows[e, h][:], y[e, h][:], g_col[:, e : e + 1], gb[e, h][:], MULT, ADD)
+        def gate_words(e, h, u, make_tile=vec_tile):
+            if u == 0:
+                c_rows[e, h] = make_tile([P, 2, P, 2], BF16, "c_rows%d_%d" % (e, h))
+            sums = y[e, h][:].rearrange("s (p u i) -> s u p i", u=2, i=2)
+            bias = gb[e, h][:].rearrange("s (u p i) -> s u p i", u=2, i=2)
+            nc.vector.scalar_tensor_tensor(c_rows[e, h][:, u], sums[:, u], small["g"][:, e : e + 1], bias[:, u], MULT, ADD)
 
         def turn(e, h):
-            pairs = c_rows[e, h][:].bitcast(F32)
-            turned = bank([P, 2, P], "turned")
+            pairs = c_rows[e, h][:].rearrange("s u p i -> s (u p i)").bitcast(F32)
+            turned[e, h] = bank([P, 2, P], "turned")
             for u in range(2):
-                nc.tensor.transpose(turned[:, u, :], pairs[:, u:256:2], ident[:])
-            c_grouped[e, h] = step_tile([P, C, 4], BF16, "c_grouped%d_%d" % (e, h))
-            nc.scalar.copy(c_grouped[e, h][:].bitcast(F32), turned[:].rearrange("p u s -> p s u"))
+                nc.tensor.transpose(turned[e, h][:, u, :], pairs[:, u * P : (u + 1) * P], ident[:])
+
+        def group_c(e, h, make_tile=act_tile):
+            c_grouped[e, h] = make_tile([P, C, 4], BF16, "c_grouped%d_%d" % (e, h))
+            nc.scalar.copy(c_grouped[e, h][:].bitcast(F32), turned[e, h][:].rearrange("p u s -> p s u"))
 
         def quantize_c(e, h):
-            c_codes[e, h] = step_tile([P, C], U32, "c_codes%d_%d" % (e, h))
+            c_codes[e, h] = vec_tile([P, C], U32, "c_codes%d_%d" % (e, h))
             c_planes[e, h] = keep_tile([P, C], U8, "c_planes%d_%d" % (e, h))
             nc.vector.quantize_mx(out=c_codes[e, h][:].bitcast(FP8X4), scales=c_planes[e, h][:], in_=c_grouped[e, h][:].rearrange("p s j -> p (s j)"))
 
-        def project_pass(e, f, h, start, stop):
+        def project_pass(sums, e, f, h, start, stop):
             cols = slice(f * P, (f + 1) * P)
             nc.tensor.matmul_mx(
-                out=o[e][:, f, :],
+                out=sums,
                 lhsT=wp_codes[h][:, cols].bitcast(FP8X4),
                 lhsT_scale=wp_planes[h][:, cols],
                 rhs=c_codes[e, h][:].bitcast(FP8X4),
@@ -235,101 +207,122 @@ def tile_moe_nxt_lin_bias_kernel(tc, x_words, x_scales, w_words, w_scales, b, wp
             )
 
         def project(e):
-            o[e] = bank([P, FT, C], "o")
+            sums = bank([P, FT, C], "o")
             for f in range(FT):
-                for h in range(HALVES):
-                    project_pass(e, f, h, h == 0, h == HALVES - 1)
+                o[e, f] = sums[:, f, :]
+                project_pass(o[e, f], e, f, 1, True, False)
+                project_pass(o[e, f], e, f, 0, False, True)
 
         def project_half(e, h):
-            if h == 0:
-                o[e] = bank([P, FT, C], "o")
             for f in range(FT):
-                project_pass(e, f, h, h == 0 and f == 0, h == HALVES - 1 and f == FT - 1)
+                if h == 0:
+                    o[e, f] = bank([P, C], "o")[:]
+                project_pass(o[e, f], e, f, h, h == 0, h == HALVES - 1)
 
-        def leave_bank(e, f):
-            o_slots[e, f] = step_tile([P, C], F32, "o_slots%d_%d" % (e, f))
-            nc.scalar.copy(o_slots[e, f][:], o[e][:, f, :])
+        def leave_half(e, f, copy, make_tile):
+            o_slots[e, f] = make_tile([P, C], F32, "o_slots%d_%d" % (e, f))
+            copy(o_slots[e, f][:], o[e, f])
 
-        def scatter(e, f):
+        def leave_rows(e, f, make_tile=act_tile):
+            leave_half(e, f, nc.scalar.copy, make_tile)
+
+        def scatter_vector(e, f=0):
             nc.vector.tensor_copy(windows[f][:].indirect(offsets[:, 8 * e : 8 * (e + 1)]), o_slots[e, f][:])
 
+        def scatter_scalar(e, f=1):
+            nc.scalar.activation(windows[f][:].indirect(offsets[:, 8 * e : 8 * (e + 1)]), o_slots[e, f][:], COPY)
+
+        load_bias()
+        load_gate(keep_tile)
+        ident = keep.tile([P, P], F32, name="ident")
+        make_identity(nc, ident[:])
+        small["zero"] = keep.tile([P, 8], F32, name="zero")
+        nc.gpsimd.memset(small["zero"][:], 0.0)
+        load_x(0, 1)
+        load_x(1, 3)
+        xs = cleared_plane(T, "xs", nc.vector.memset)
+        load_scale_rows(xs, x_scales)
+        w_planes[0] = cleared_plane(N, "ws0", nc.vector.memset)
+        load_scale_rows(w_planes[0], w_scales[0])
+        w_planes[1] = cleared_plane(N, "ws1", nc.vector.memset)
+        load_w(0, 0)
+        load_wp(0)
+        load_w(0, 1)
+        load_wp(1)
+        load_w(0, 2)
+        load_scale_rows(w_planes[1], w_scales[1])
+        load_w(1, 0)
+
+        clear_window(0)
+        clear_window(1)
         turn_gate()
-        spread_bias(0)
-        gated_bias(0)
-        spread_bias(1)
-        gated_bias(1)
-        spread_bias(2)
-        gated_bias(2)
-        spread_bias(3)
-        gated_bias(3)
+        for e in range(E):
+            spread_bias(e)
+            gated_bias(e)
         gather_words(0, 0)
+        gather_words(1, 0)
+        gather_words(0, 1)
         gather_scales(0, 0)
         gather_scales(0, 1)
-        gather_scales(0, 2)
-        gather_words(0, 1)
         gather_words(0, 2)
-        gather_scales(1, 0)
-        gather_scales(1, 1)
-        gather_scales(1, 2)
-        gather_words(1, 0)
-        gather_words(1, 1)
-        gather_words(1, 2)
-        multiply_by_pass(0)
-        gate_and_bias(0, 0)
-        gate_and_bias(0, 1)
-        multiply_by_pass(1)
-        gate_and_bias(1, 0)
-        gate_and_bias(1, 1)
-        group_wp(0, nc.scalar.copy)
-        turn(0, 0)
-        turn(0, 1)
-        turn(1, 0)
-        turn(1, 1)
-        group_wp(1, nc.vector.tensor_copy)
+        gather_scales(0, 2)
+        for a in range(1, PASSES):
+            gather_words(1, a)
+        for a in range(PASSES):
+            gather_scales(1, a)
+        group_wp(0, nc.scalar.copy, act_tile)
+        group_wp(1, nc.vector.tensor_copy, vec_tile)
         quantize_wp(0)
+
+        first_pass(0)
+        later_passes(0)
+        gate_words(0, 0, 0)
         quantize_wp(1)
-        quantize_c(0, 0)
-        quantize_c(0, 1)
-        project(0)
-        quantize_c(1, 0)
-        quantize_c(1, 1)
-        project(1)
-        leave_bank(0, 0)
-        scatter(0, 0)
-        leave_bank(0, 1)
-        scatter(0, 1)
-        leave_bank(1, 0)
-        scatter(1, 0)
-        multiply_by_pass(2, 0, 1)
-        multiply_by_pass(2, 1, 2)
-        multiply_by_pass(3, 0, 1)
-        multiply_by_pass(2, 2, 3)
-        gate_and_bias(2, 0)
-        gate_and_bias(2, 1)
-        multiply_by_pass(3, 1, 2)
-        multiply_by_pass(3, 2, 3)
-        gate_and_bias(3, 0)
-        gate_and_bias(3, 1)
-        turn(2, 0)
-        turn(2, 1)
-        quantize_c(2, 0)
-        leave_bank(1, 1)
-        quantize_c(2, 1)
-        turn(3, 0)
-        turn(3, 1)
-        project(2)
-        scatter(1, 1)
-        quantize_c(3, 0)
-        leave_bank(2, 0)
-        leave_bank(2, 1)
-        quantize_c(3, 1)
-        project(3)
-        scatter(2, 0)
-        scatter(2, 1)
-        leave_bank(3, 0)
-        leave_bank(3, 1)
-        scatter(3, 0)
-        scatter(3, 1)
+        gate_words(0, 0, 1)
+        gate_words(0, 1, 0)
+        gate_words(0, 1, 1)
+        for e in range(1, E):
+            first_pass(e)
+            turn(e - 1, 0)
+            turn(e - 1, 1)
+            group_c(e - 1, 0)
+            group_c(e - 1, 1, load_tile)
+            if e > 1:
+                leave_rows(e - 2, 1)
+                scatter_scalar(e - 2)
+            load_w(e, 1)
+            load_w(e, 2)
+            if e + 1 < E:
+                w_planes[e + 1] = cleared_plane(N, "ws%d" % (e + 1), nc.gpsimd.memset)
+                load_scale_rows(w_planes[e + 1], w_scales[e + 1])
+                load_w(e + 1, 0)
+            later_passes(e)
+            quantize_c(e - 1, 0)
+            gate_words(e, 0, 0)
+            quantize_c(e - 1, 1)
+            project(e - 1)
+            gate_words(e, 0, 1)
+            gate_words(e, 1, 0)
+            gate_words(e, 1, 1)
+            if e + 1 < E:
+                leave_rows(e - 1, 0)
+                scatter_vector(e - 1)
+        last = E - 1
+        turn(last, 0)
+        turn(last, 1)
+        group_c(last, 0)
+        group_c(last, 1)
+        leave_rows(last - 1, 0)
+        leave_rows(last - 1, 1)
+        for h in range(HALVES):
+            quantize_c(last, h)
+            project_half(last, h)
+        scatter_vector(last - 1)
+        scatter_scalar(last - 1)
+        leave_half(last, 0, nc.vector.tensor_copy, vec_tile)
+        leave_half(last, 1, nc.scalar.copy, act_tile)
+        scatter_vector(last)
+        scatter_scalar(last)
 
         nc.sync.dma_start(out[0:P, :], windows[0][:])
         nc.scalar.dma_start(out[P : 2 * P, :], windows[1][:])

@@ -31,7 +31,7 @@ def tile_moe_nxt_lin_bias_kernel(tc, x_words, x_scales, w_words, w_scales, b, wp
         keep = ctx.enter_context(tc.tile_pool(name="keep", bufs=1))
         loads = ctx.enter_context(tc.tile_pool(name="loads", bufs=22))
         vec = ctx.enter_context(tc.tile_pool(name="vec", bufs=32))
-        act = ctx.enter_context(tc.tile_pool(name="act", bufs=30))
+        act = ctx.enter_context(tc.tile_pool(name="act", bufs=24))
         psum = ctx.enter_context(tc.psum_pool(name="psum", bufs=8))
 
         offsets = keep.tile([P, E * C // 16], U16, name="offsets")
@@ -84,8 +84,8 @@ def tile_moe_nxt_lin_bias_kernel(tc, x_words, x_scales, w_words, w_scales, b, wp
             for r in range(4):
                 nc.sync.dma_start(plane[r:P:32].bitcast(I32), rows[r].bitcast(I32))
 
-        def load_x(first, last):
-            tile = keep.tile([P, last - first, T], I32, name="xw%d" % first, align_bytes=256)
+        def load_x(first, last, make_tile):
+            tile = make_tile([P, last - first, T], I32, "xw%d" % first)
             nc.sync.dma_start(tile[:], x_words[first:last].rearrange("a p t r -> p a (t r)").bitcast(I32))
             for a in range(first, last):
                 x_windows[a] = tile[:, a - first, :]
@@ -166,6 +166,9 @@ def tile_moe_nxt_lin_bias_kernel(tc, x_words, x_scales, w_words, w_scales, b, wp
                 y[e, h] = bank([P, 512], "y")
                 multiply(e, 0, h, True, False)
 
+        def one_pass(e, a, h):
+            multiply(e, a, h, False, a == PASSES - 1)
+
         def later_passes(e):
             multiply(e, 1, 0, False, False)
             multiply(e, 2, 0, False, True)
@@ -213,6 +216,12 @@ def tile_moe_nxt_lin_bias_kernel(tc, x_words, x_scales, w_words, w_scales, b, wp
                 project_pass(o[e, f], e, f, 1, True, False)
                 project_pass(o[e, f], e, f, 0, False, True)
 
+        def project_apart(e):
+            for f in range(FT):
+                o[e, f] = bank([P, C], "o")[:]
+                project_pass(o[e, f], e, f, 1, True, False)
+                project_pass(o[e, f], e, f, 0, False, True)
+
         def project_half(e, h):
             for f in range(FT):
                 if h == 0:
@@ -238,91 +247,118 @@ def tile_moe_nxt_lin_bias_kernel(tc, x_words, x_scales, w_words, w_scales, b, wp
         make_identity(nc, ident[:])
         small["zero"] = keep.tile([P, 8], F32, name="zero")
         nc.gpsimd.memset(small["zero"][:], 0.0)
-        load_x(0, 1)
-        load_x(1, 3)
+        load_x(0, 1, keep_tile)
         xs = cleared_plane(T, "xs", nc.vector.memset)
         load_scale_rows(xs, x_scales)
         w_planes[0] = cleared_plane(N, "ws0", nc.vector.memset)
-        load_scale_rows(w_planes[0], w_scales[0])
+        load_x(1, 3, load_tile)
         w_planes[1] = cleared_plane(N, "ws1", nc.vector.memset)
-        load_w(0, 0)
+        for e in range(2):
+            load_scale_rows(w_planes[e], w_scales[e])
+        windows[0] = load_tile([P, T], F32, "window0")
+        nc.vector.memset(windows[0][:].bitcast(I32), 0)
+        load_expert(0)
         load_wp(0)
-        load_w(0, 1)
-        load_wp(1)
-        load_w(0, 2)
-        load_scale_rows(w_planes[1], w_scales[1])
         load_w(1, 0)
+        load_w(1, 1)
 
-        clear_window(0)
         clear_window(1)
         turn_gate()
         for e in range(E):
             spread_bias(e)
             gated_bias(e)
-        gather_words(0, 0)
-        gather_words(1, 0)
-        gather_words(0, 1)
-        gather_scales(0, 0)
-        gather_scales(0, 1)
-        gather_words(0, 2)
-        gather_scales(0, 2)
-        for a in range(1, PASSES):
-            gather_words(1, a)
-        for a in range(PASSES):
-            gather_scales(1, a)
-        group_wp(0, nc.scalar.copy, act_tile)
-        group_wp(1, nc.vector.tensor_copy, vec_tile)
-        quantize_wp(0)
+        for i in range(2):
+            gather_words(i, 0)
+            for a in range(PASSES):
+                gather_scales(i, a)
+            gather_words(i, 1)
+            gather_words(i, 2)
+
+        def gate_half(e, h):
+            for u in range(2):
+                gate_words(e, h, u)
+
+        def turn_half(e, h):
+            turn(e, h)
+            group_c(e, h)
+
+        def both_halves(e, a):
+            for h in range(HALVES):
+                one_pass(e, a, h)
 
         first_pass(0)
         later_passes(0)
-        gate_words(0, 0, 0)
+        gate_half(0, 0)
+        gate_half(0, 1)
+        group_wp(0, nc.scalar.copy, act_tile)
+        first_pass(1)
+        both_halves(1, 1)
+        turn_half(0, 0)
+        turn(0, 1)
+        group_c(0, 1, load_tile)
+        load_wp(1)
+        load_w(1, 2)
+        for e in range(2, E):
+            w_planes[e] = cleared_plane(N, "ws%d" % e, nc.gpsimd.memset)
+        for e in range(2, E):
+            load_scale_rows(w_planes[e], w_scales[e])
+        load_w(2, 0)
+        load_w(2, 1)
+        load_w(3, 0)
+        load_w(2, 2)
+        load_w(3, 1)
+        load_w(3, 2)
+        quantize_wp(0)
+        group_wp(1, nc.vector.tensor_copy, vec_tile)
+        quantize_c(0, 0)
         quantize_wp(1)
-        gate_words(0, 0, 1)
-        gate_words(0, 1, 0)
-        gate_words(0, 1, 1)
-        for e in range(1, E):
-            first_pass(e)
-            turn(e - 1, 0)
-            turn(e - 1, 1)
-            group_c(e - 1, 0)
-            group_c(e - 1, 1, load_tile)
-            if e > 1:
-                leave_rows(e - 2, 1)
-                scatter_scalar(e - 2)
-            load_w(e, 1)
-            load_w(e, 2)
-            if e + 1 < E:
-                w_planes[e + 1] = cleared_plane(N, "ws%d" % (e + 1), nc.gpsimd.memset)
-                load_scale_rows(w_planes[e + 1], w_scales[e + 1])
-                load_w(e + 1, 0)
-            later_passes(e)
-            quantize_c(e - 1, 0)
-            gate_words(e, 0, 0)
-            quantize_c(e - 1, 1)
-            project(e - 1)
-            gate_words(e, 0, 1)
-            gate_words(e, 1, 0)
-            gate_words(e, 1, 1)
-            if e + 1 < E:
-                leave_rows(e - 1, 0)
-                scatter_vector(e - 1)
-        last = E - 1
-        turn(last, 0)
-        turn(last, 1)
-        group_c(last, 0)
-        group_c(last, 1)
-        leave_rows(last - 1, 0)
-        leave_rows(last - 1, 1)
-        for h in range(HALVES):
-            quantize_c(last, h)
-            project_half(last, h)
-        scatter_vector(last - 1)
-        scatter_scalar(last - 1)
-        leave_half(last, 0, nc.vector.tensor_copy, vec_tile)
-        leave_half(last, 1, nc.scalar.copy, act_tile)
-        scatter_vector(last)
-        scatter_scalar(last)
+        both_halves(1, 2)
+        quantize_c(0, 1)
+        gate_half(1, 0)
+        gate_half(1, 1)
+        project(0)
+        leave_rows(0, 0)
+        turn_half(1, 0)
+        turn_half(1, 1)
+        leave_rows(0, 1)
+        scatter_vector(0)
+        scatter_scalar(0)
+        quantize_c(1, 0)
+        quantize_c(1, 1)
+        first_pass(2)
+        both_halves(2, 1)
+        project(1)
+        leave_rows(1, 0)
+        leave_rows(1, 1)
+        scatter_scalar(1, 0)
+        scatter_scalar(1, 1)
+        first_pass(3)
+        both_halves(2, 2)
+        gate_half(2, 0)
+        gate_half(2, 1)
+        both_halves(3, 1)
+        both_halves(3, 2)
+        gate_half(3, 0)
+        gate_half(3, 1)
+        turn_half(2, 0)
+        turn_half(2, 1)
+        turn_half(3, 0)
+        turn_half(3, 1)
+        quantize_c(2, 0)
+        quantize_c(2, 1)
+        project_apart(2)
+        leave_half(2, 0, nc.scalar.copy, act_tile)
+        leave_half(2, 1, nc.scalar.copy, act_tile)
+        quantize_c(3, 0)
+        project_half(3, 0)
+        quantize_c(3, 1)
+        project_half(3, 1)
+        scatter_vector(2)
+        scatter_scalar(2)
+        leave_half(3, 0, nc.vector.tensor_copy, vec_tile)
+        leave_half(3, 1, nc.scalar.copy, act_tile)
+        scatter_vector(3)
+        scatter_scalar(3)
 
         nc.sync.dma_start(out[0:P, :], windows[0][:])
         nc.scalar.dma_start(out[P : 2 * P, :], windows[1][:])

@@ -30,8 +30,8 @@ def tile_moe_nxt_lin_bias_kernel(tc, x_words, x_scales, w_words, w_scales, b, wp
     with ExitStack() as ctx:
         keep = ctx.enter_context(tc.tile_pool(name="keep", bufs=1))
         loads = ctx.enter_context(tc.tile_pool(name="loads", bufs=22))
-        vec = ctx.enter_context(tc.tile_pool(name="vec", bufs=32))
-        act = ctx.enter_context(tc.tile_pool(name="act", bufs=24))
+        vec = ctx.enter_context(tc.tile_pool(name="vec", bufs=33))
+        act = ctx.enter_context(tc.tile_pool(name="act", bufs=23))
         psum = ctx.enter_context(tc.psum_pool(name="psum", bufs=8))
 
         offsets = keep.tile([P, E * C // 16], U16, name="offsets")
@@ -109,6 +109,11 @@ def tile_moe_nxt_lin_bias_kernel(tc, x_words, x_scales, w_words, w_scales, b, wp
         def load_gate(make_tile):
             small["g_rows"] = make_tile([P, C], F32, "g_rows")
             nc.scalar.dma_start(small["g_rows"][:], gate.rearrange("r (e s) -> (r e) s", s=C)[0:P])
+
+        def load_gate_rows():
+            small["g_rows"] = keep_tile([P, C], F32, "g_rows")
+            nc.gpsimd.memset(small["g_rows"][:], 0.0)
+            nc.scalar.dma_start(small["g_rows"][0:E, :], gate[0].rearrange("(e s) -> e s", s=C))
 
         def clear_window(f):
             windows[f] = keep.tile([P, T], F32, name="window%d" % f)
@@ -235,6 +240,14 @@ def tile_moe_nxt_lin_bias_kernel(tc, x_words, x_scales, w_words, w_scales, b, wp
         def leave_rows(e, f, make_tile=act_tile):
             leave_half(e, f, nc.scalar.copy, make_tile)
 
+        def leave_into_pair(e, f):
+            if e % 2 == 0:
+                o_slots["pair", f] = act_tile([P, 2, C], F32, "o_pair%d" % f)
+            nc.scalar.copy(o_slots["pair", f][:, e % 2, :], o[e, f])
+
+        def scatter_pair(e, f):
+            nc.scalar.activation(windows[f][:].indirect(offsets[:, 8 * e : 8 * (e + 2)]), o_slots["pair", f][:].rearrange("p a s -> p (a s)"), COPY)
+
         def scatter_vector(e, f=0):
             nc.vector.tensor_copy(windows[f][:].indirect(offsets[:, 8 * e : 8 * (e + 1)]), o_slots[e, f][:])
 
@@ -326,12 +339,13 @@ def tile_moe_nxt_lin_bias_kernel(tc, x_words, x_scales, w_words, w_scales, b, wp
         quantize_c(1, 0)
         quantize_c(1, 1)
         first_pass(2)
-        both_halves(2, 1)
-        project(1)
-        leave_rows(1, 0)
-        leave_rows(1, 1)
-        scatter_scalar(1, 0)
-        scatter_scalar(1, 1)
+        one_pass(2, 1, 0)
+        project_apart(1)
+        one_pass(2, 1, 1)
+        leave_half(1, 0, nc.vector.tensor_copy, vec_tile)
+        leave_half(1, 1, nc.scalar.copy, act_tile)
+        scatter_vector(1)
+        scatter_scalar(1)
         first_pass(3)
         both_halves(2, 2)
         gate_half(2, 0)

@@ -29,9 +29,9 @@ def tile_moe_nxt_lin_bias_kernel(tc, x_words, x_scales, w_words, w_scales, b, wp
     nc = tc.nc
     with ExitStack() as ctx:
         keep = ctx.enter_context(tc.tile_pool(name="keep", bufs=1))
-        loads = ctx.enter_context(tc.tile_pool(name="loads", bufs=22))
-        vec = ctx.enter_context(tc.tile_pool(name="vec", bufs=33))
-        act = ctx.enter_context(tc.tile_pool(name="act", bufs=23))
+        loads = ctx.enter_context(tc.tile_pool(name="loads", bufs=23))
+        vec = ctx.enter_context(tc.tile_pool(name="vec", bufs=35))
+        act = ctx.enter_context(tc.tile_pool(name="act", bufs=25))
         psum = ctx.enter_context(tc.psum_pool(name="psum", bufs=8))
 
         offsets = keep.tile([P, E * C // 16], U16, name="offsets")
@@ -84,6 +84,22 @@ def tile_moe_nxt_lin_bias_kernel(tc, x_words, x_scales, w_words, w_scales, b, wp
             for r in range(4):
                 nc.sync.dma_start(plane[r:P:32].bitcast(I32), rows[r].bitcast(I32))
 
+        def load_scale_rows_five(plane, scales):
+            rows = scales.rearrange("a (q r) n -> r q a n", r=4)
+            for r in range(3):
+                nc.sync.dma_start(plane[r:P:32].bitcast(I32), rows[r].bitcast(I32))
+            nc.sync.dma_start(plane[3:P:32, 0:2].bitcast(I32), rows[3][:, 0:2].bitcast(I32))
+            nc.sync.dma_start(plane[3:P:32, 2].bitcast(I32), rows[3][:, 2].bitcast(I32))
+
+        def load_scale_rows_six(plane, scales):
+            rows = scales.rearrange("a (q r) n -> r q a n", r=4)
+            for r in range(2):
+                nc.sync.dma_start(plane[r:P:32].bitcast(I32), rows[r].bitcast(I32))
+            for r in range(2, 4):
+                nc.sync.dma_start(plane[r:P:32, 0:2].bitcast(I32), rows[r][:, 0:2].bitcast(I32))
+            for r in range(2, 4):
+                nc.sync.dma_start(plane[r:P:32, 2].bitcast(I32), rows[r][:, 2].bitcast(I32))
+
         def load_x(first, last, make_tile):
             tile = make_tile([P, last - first, T], I32, "xw%d" % first)
             nc.sync.dma_start(tile[:], x_words[first:last].rearrange("a p t r -> p a (t r)").bitcast(I32))
@@ -91,8 +107,21 @@ def tile_moe_nxt_lin_bias_kernel(tc, x_words, x_scales, w_words, w_scales, b, wp
                 x_windows[a] = tile[:, a - first, :]
 
         def load_w(e, a):
-            ww[e, a] = load_tile([P, 2 * N], U8, "ww%d_%d" % (e, a))
-            nc.sync.dma_start(ww[e, a][:].bitcast(I32), w_words[e, a].bitcast(I32))
+            tile = load_tile([P, 2 * N], U8, "ww%d_%d" % (e, a))
+            nc.sync.dma_start(tile[:].bitcast(I32), w_words[e, a].bitcast(I32))
+            for h in range(HALVES):
+                ww[e, a, h] = tile[:, N * h : N * (h + 1)]
+
+        def load_half(e, a, h):
+            tile = load_tile([P, N], U8, "ww%d_%d_%d" % (e, a, h))
+            nc.sync.dma_start(tile[:].bitcast(I32), w_words[e, a][:, N * h : N * (h + 1)].bitcast(I32))
+            ww[e, a, h] = tile[:]
+
+        def load_last_in_halves(e):
+            for a in range(PASSES - 1):
+                load_w(e, a)
+            for h in range(HALVES):
+                load_half(e, PASSES - 1, h)
 
         def load_expert(e):
             for a in range(PASSES):
@@ -116,7 +145,7 @@ def tile_moe_nxt_lin_bias_kernel(tc, x_words, x_scales, w_words, w_scales, b, wp
             nc.scalar.dma_start(small["g_rows"][0:E, :], gate[0].rearrange("(e s) -> e s", s=C))
 
         def clear_window(f):
-            windows[f] = keep.tile([P, T], F32, name="window%d" % f)
+            windows[f] = act_tile([P, T], F32, "window%d" % f)
             nc.scalar.activation(windows[f][:], small["zero"][:, 0:1].to_broadcast([P, T]), COPY)
 
         def turn_gate():
@@ -144,14 +173,20 @@ def tile_moe_nxt_lin_bias_kernel(tc, x_words, x_scales, w_words, w_scales, b, wp
                 gb[e, h] = act_tile([P, 512], F32, "gb%d_%d" % (e, h))
                 nc.scalar.activation(gb[e, h][:].rearrange("s (u p i) -> s u p i", u=2, i=2), spread[e, h][:].rearrange("s (u i) p -> s u p i", u=2), COPY, scale=small["g"][:, e : e + 1])
 
-        def group_wp(h, copy, make_tile):
-            wp_grouped[h] = make_tile([P, M, 4], BF16, "wp_grouped%d" % h)
-            copy(wp_grouped[h][:].rearrange("p (c i) j -> p c j i", i=4), wp_raw[h][:].rearrange("p j (c i) -> p c j i", i=4))
+        def group_wp(h, copy, make_tile, cols):
+            grouped = make_tile([P, cols.stop - cols.start, 4], BF16, "wp_grouped%d_%d" % (h, cols.start))
+            copy(grouped[:].rearrange("p (c i) j -> p c j i", i=4), wp_raw[h][:, :, cols].rearrange("p j (c i) -> p c j i", i=4))
+            wp_grouped[h, cols.start] = grouped
 
-        def quantize_wp(h):
-            wp_codes[h] = vec_tile([P, M], U32, "wp_codes%d" % h)
-            wp_planes[h] = keep_tile([P, M], U8, "wp_planes%d" % h)
-            nc.vector.quantize_mx(out=wp_codes[h][:].bitcast(FP8X4), scales=wp_planes[h][:], in_=wp_grouped[h][:].rearrange("p f j -> p (f j)"))
+        def quantize_wp(h, first):
+            grouped = wp_grouped[h, first]
+            width = grouped.shape[1]
+            codes = vec_tile([P, width], U32, "wp_codes%d_%d" % (h, first))
+            plane = keep_tile([P, width], U8, "wp_planes%d_%d" % (h, first))
+            nc.vector.quantize_mx(out=codes[:].bitcast(FP8X4), scales=plane[:], in_=grouped[:].rearrange("p f j -> p (f j)"))
+            for at in range(0, width, P):
+                wp_codes[h, (first + at) // P] = codes[:, at : at + P]
+                wp_planes[h, (first + at) // P] = plane[:, at : at + P]
 
         def multiply(e, a, h, start, stop):
             i, s = divmod(e, 2)
@@ -160,7 +195,7 @@ def tile_moe_nxt_lin_bias_kernel(tc, x_words, x_scales, w_words, w_scales, b, wp
                 out=y[e, h][:],
                 lhsT=gw[i, a][:, slots].bitcast(FP8X4),
                 lhsT_scale=gs[i, a][:, slots],
-                rhs=ww[e, a][:, N * h : N * (h + 1)].bitcast(FP4X4),
+                rhs=ww[e, a, h].bitcast(FP4X4),
                 rhs_scale=w_planes[e][:, a, 512 * h : 512 * (h + 1)],
                 start=start,
                 stop=stop,
@@ -173,6 +208,11 @@ def tile_moe_nxt_lin_bias_kernel(tc, x_words, x_scales, w_words, w_scales, b, wp
 
         def one_pass(e, a, h):
             multiply(e, a, h, False, a == PASSES - 1)
+
+        def later_by_halves(e):
+            for h in range(HALVES):
+                for a in range(1, PASSES):
+                    one_pass(e, a, h)
 
         def later_passes(e):
             multiply(e, 1, 0, False, False)
@@ -199,15 +239,15 @@ def tile_moe_nxt_lin_bias_kernel(tc, x_words, x_scales, w_words, w_scales, b, wp
 
         def quantize_c(e, h):
             c_codes[e, h] = vec_tile([P, C], U32, "c_codes%d_%d" % (e, h))
-            c_planes[e, h] = keep_tile([P, C], U8, "c_planes%d_%d" % (e, h))
+            if (e, h) not in c_planes:
+                c_planes[e, h] = keep_tile([P, C], U8, "c_planes%d_%d" % (e, h))
             nc.vector.quantize_mx(out=c_codes[e, h][:].bitcast(FP8X4), scales=c_planes[e, h][:], in_=c_grouped[e, h][:].rearrange("p s j -> p (s j)"))
 
         def project_pass(sums, e, f, h, start, stop):
-            cols = slice(f * P, (f + 1) * P)
             nc.tensor.matmul_mx(
                 out=sums,
-                lhsT=wp_codes[h][:, cols].bitcast(FP8X4),
-                lhsT_scale=wp_planes[h][:, cols],
+                lhsT=wp_codes[h, f].bitcast(FP8X4),
+                lhsT_scale=wp_planes[h, f],
                 rhs=c_codes[e, h][:].bitcast(FP8X4),
                 rhs_scale=c_planes[e, h][:],
                 start=start,
@@ -258,8 +298,6 @@ def tile_moe_nxt_lin_bias_kernel(tc, x_words, x_scales, w_words, w_scales, b, wp
         load_gate(keep_tile)
         ident = keep.tile([P, P], F32, name="ident")
         make_identity(nc, ident[:])
-        small["zero"] = keep.tile([P, 8], F32, name="zero")
-        nc.gpsimd.memset(small["zero"][:], 0.0)
         load_x(0, 1, keep_tile)
         xs = cleared_plane(T, "xs", nc.vector.memset)
         load_scale_rows(xs, x_scales)
@@ -268,24 +306,26 @@ def tile_moe_nxt_lin_bias_kernel(tc, x_words, x_scales, w_words, w_scales, b, wp
         w_planes[1] = cleared_plane(N, "ws1", nc.vector.memset)
         for e in range(2):
             load_scale_rows(w_planes[e], w_scales[e])
-        windows[0] = load_tile([P, T], F32, "window0")
-        nc.vector.memset(windows[0][:].bitcast(I32), 0)
+        small["zero"] = load_tile([P, 8], F32, "zero")
+        nc.vector.memset(small["zero"][:], 0.0)
         load_expert(0)
         load_wp(0)
         load_w(1, 0)
-        load_w(1, 1)
+        load_wp(1)
 
-        clear_window(1)
         turn_gate()
         for e in range(E):
             spread_bias(e)
             gated_bias(e)
-        for i in range(2):
-            gather_words(i, 0)
-            for a in range(PASSES):
-                gather_scales(i, a)
-            gather_words(i, 1)
-            gather_words(i, 2)
+        gather_words(0, 0)
+        for a in range(PASSES):
+            gather_scales(0, a)
+        gather_words(0, 1)
+        gather_words(0, 2)
+        for a in range(PASSES):
+            gather_words(1, a)
+        for a in range(PASSES - 1):
+            gather_scales(1, a)
 
         def gate_half(e, h):
             for u in range(2):
@@ -303,28 +343,33 @@ def tile_moe_nxt_lin_bias_kernel(tc, x_words, x_scales, w_words, w_scales, b, wp
         later_passes(0)
         gate_half(0, 0)
         gate_half(0, 1)
-        group_wp(0, nc.scalar.copy, act_tile)
+        group_wp(0, nc.scalar.copy, act_tile, slice(0, M))
         first_pass(1)
-        both_halves(1, 1)
         turn_half(0, 0)
         turn(0, 1)
         group_c(0, 1, load_tile)
-        load_wp(1)
+        for f in range(FT):
+            clear_window(f)
+        load_w(1, 1)
         load_w(1, 2)
         for e in range(2, E):
             w_planes[e] = cleared_plane(N, "ws%d" % e, nc.gpsimd.memset)
         for e in range(2, E):
             load_scale_rows(w_planes[e], w_scales[e])
         load_w(2, 0)
+        c_planes[0, 1] = load_tile([P, C], U8, "c_planes0_1")
         load_w(2, 1)
         load_w(3, 0)
         load_w(2, 2)
         load_w(3, 1)
         load_w(3, 2)
-        quantize_wp(0)
-        group_wp(1, nc.vector.tensor_copy, vec_tile)
+        quantize_wp(0, 0)
+        for f in range(FT):
+            group_wp(1, nc.vector.tensor_copy, vec_tile, slice(f * P, (f + 1) * P))
         quantize_c(0, 0)
-        quantize_wp(1)
+        for f in range(FT):
+            quantize_wp(1, f * P)
+        both_halves(1, 1)
         both_halves(1, 2)
         quantize_c(0, 1)
         gate_half(1, 0)
@@ -338,6 +383,7 @@ def tile_moe_nxt_lin_bias_kernel(tc, x_words, x_scales, w_words, w_scales, b, wp
         scatter_scalar(0)
         quantize_c(1, 0)
         quantize_c(1, 1)
+        gather_scales(1, 2)
         first_pass(2)
         one_pass(2, 1, 0)
         project_apart(1)

@@ -29,9 +29,9 @@ def tile_moe_nxt_lin_bias_kernel(tc, x_words, x_scales, w_words, w_scales, b, wp
     nc = tc.nc
     with ExitStack() as ctx:
         keep = ctx.enter_context(tc.tile_pool(name="keep", bufs=1))
-        loads = ctx.enter_context(tc.tile_pool(name="loads", bufs=23))
-        vec = ctx.enter_context(tc.tile_pool(name="vec", bufs=35))
-        act = ctx.enter_context(tc.tile_pool(name="act", bufs=25))
+        loads = ctx.enter_context(tc.tile_pool(name="loads", bufs=25))
+        vec = ctx.enter_context(tc.tile_pool(name="vec", bufs=36))
+        act = ctx.enter_context(tc.tile_pool(name="act", bufs=27))
         psum = ctx.enter_context(tc.psum_pool(name="psum", bufs=8))
 
         offsets = keep.tile([P, E * C // 16], U16, name="offsets")
@@ -74,31 +74,17 @@ def tile_moe_nxt_lin_bias_kernel(tc, x_words, x_scales, w_words, w_scales, b, wp
         o_slots = {}
         small = {}
 
-        def cleared_plane(width, name, memset):
-            plane = load_tile([P, PASSES, width], U8, name)
+        def cleared_plane(shape, name, memset):
+            plane = load_tile(shape, U8, name)
             memset(plane[:].rearrange("p a n -> p (a n)").bitcast(I32), 0)
             return plane
 
-        def load_scale_rows(plane, scales):
+        def load_scale_rows(plane, scales, cuts):
             rows = scales.rearrange("a (q r) n -> r q a n", r=4)
             for r in range(4):
-                nc.sync.dma_start(plane[r:P:32].bitcast(I32), rows[r].bitcast(I32))
-
-        def load_scale_rows_five(plane, scales):
-            rows = scales.rearrange("a (q r) n -> r q a n", r=4)
-            for r in range(3):
-                nc.sync.dma_start(plane[r:P:32].bitcast(I32), rows[r].bitcast(I32))
-            nc.sync.dma_start(plane[3:P:32, 0:2].bitcast(I32), rows[3][:, 0:2].bitcast(I32))
-            nc.sync.dma_start(plane[3:P:32, 2].bitcast(I32), rows[3][:, 2].bitcast(I32))
-
-        def load_scale_rows_six(plane, scales):
-            rows = scales.rearrange("a (q r) n -> r q a n", r=4)
-            for r in range(2):
-                nc.sync.dma_start(plane[r:P:32].bitcast(I32), rows[r].bitcast(I32))
-            for r in range(2, 4):
-                nc.sync.dma_start(plane[r:P:32, 0:2].bitcast(I32), rows[r][:, 0:2].bitcast(I32))
-            for r in range(2, 4):
-                nc.sync.dma_start(plane[r:P:32, 2].bitcast(I32), rows[r][:, 2].bitcast(I32))
+                edges = [0] + cuts[r] + [plane.shape[1]]
+                for first, last in zip(edges, edges[1:]):
+                    nc.sync.dma_start(plane[r:P:32, first:last].bitcast(I32), rows[r][:, first:last].bitcast(I32))
 
         def load_x(first, last, make_tile):
             tile = make_tile([P, last - first, T], I32, "xw%d" % first)
@@ -112,20 +98,11 @@ def tile_moe_nxt_lin_bias_kernel(tc, x_words, x_scales, w_words, w_scales, b, wp
             for h in range(HALVES):
                 ww[e, a, h] = tile[:, N * h : N * (h + 1)]
 
-        def load_half(e, a, h):
-            tile = load_tile([P, N], U8, "ww%d_%d_%d" % (e, a, h))
-            nc.sync.dma_start(tile[:].bitcast(I32), w_words[e, a][:, N * h : N * (h + 1)].bitcast(I32))
-            ww[e, a, h] = tile[:]
-
-        def load_last_in_halves(e):
-            for a in range(PASSES - 1):
-                load_w(e, a)
-            for h in range(HALVES):
-                load_half(e, PASSES - 1, h)
-
-        def load_expert(e):
-            for a in range(PASSES):
-                load_w(e, a)
+        def load_half(e, first, last, h):
+            tile = load_tile([P, last - first, N], U8, "ww%d_%d_%d" % (e, first, h))
+            nc.sync.dma_start(tile[:].bitcast(I32), w_words[e, first:last].rearrange("a p n -> p a n")[:, :, N * h : N * (h + 1)].bitcast(I32))
+            for a in range(first, last):
+                ww[e, a, h] = tile[:, a - first, :]
 
         def load_wp(h):
             wp_raw[h] = load_tile([P, 4, M], F32, "wp_raw%d" % h)
@@ -135,14 +112,9 @@ def tile_moe_nxt_lin_bias_kernel(tc, x_words, x_scales, w_words, w_scales, b, wp
             small["b"] = keep.tile([P, HALVES, 4, E], F32, name="b_col")
             nc.scalar.dma_start(small["b"][:], b.rearrange("(h p j) e -> p h j e", h=HALVES, j=4))
 
-        def load_gate(make_tile):
-            small["g_rows"] = make_tile([P, C], F32, "g_rows")
-            nc.scalar.dma_start(small["g_rows"][:], gate.rearrange("r (e s) -> (r e) s", s=C)[0:P])
-
-        def load_gate_rows():
+        def load_gate():
             small["g_rows"] = keep_tile([P, C], F32, "g_rows")
-            nc.gpsimd.memset(small["g_rows"][:], 0.0)
-            nc.scalar.dma_start(small["g_rows"][0:E, :], gate[0].rearrange("(e s) -> e s", s=C))
+            nc.scalar.dma_start(small["g_rows"][:], gate.rearrange("r (e s) -> (r e) s", s=C)[0:P])
 
         def clear_window(f):
             windows[f] = act_tile([P, T], F32, "window%d" % f)
@@ -154,13 +126,17 @@ def tile_moe_nxt_lin_bias_kernel(tc, x_words, x_scales, w_words, w_scales, b, wp
             small["g"] = act_tile([P, E], F32, "g_col")
             nc.scalar.copy(small["g"][:], g_turned[:, 0:E])
 
-        def gather_scales(i, a):
-            gs[i, a] = vec_tile([P, 2 * C], U8, "gs%d_%d" % (i, a))
-            nc.vector.tensor_copy(gs[i, a][:], xs[:, a, :].indirect(offsets[:, 16 * i : 16 * (i + 1)]))
+        def gather_scales(first, last, a):
+            tile = vec_tile([P, (last - first) * C], U8, "gs%d_%d" % (first, a))
+            nc.vector.tensor_copy(tile[:], xs[:, a, :].indirect(offsets[:, 8 * first : 8 * last]))
+            for e in range(first, last):
+                gs[e, a] = tile[:, (e - first) * C : (e - first + 1) * C]
 
-        def gather_words(i, a, make_tile=vec_tile):
-            gw[i, a] = make_tile([P, 2 * C], U32, "gw%d_%d" % (i, a))
-            nc.vector.tensor_copy(gw[i, a][:], x_windows[a].bitcast(U32).indirect(offsets[:, 16 * i : 16 * (i + 1)]))
+        def gather_words(first, last, a):
+            tile = vec_tile([P, (last - first) * C], U32, "gw%d_%d" % (first, a))
+            nc.vector.tensor_copy(tile[:], x_windows[a].bitcast(U32).indirect(offsets[:, 8 * first : 8 * last]))
+            for e in range(first, last):
+                gw[e, a] = tile[:, (e - first) * C : (e - first + 1) * C]
 
         def spread_bias(e):
             for h in range(HALVES):
@@ -189,12 +165,10 @@ def tile_moe_nxt_lin_bias_kernel(tc, x_words, x_scales, w_words, w_scales, b, wp
                 wp_planes[h, (first + at) // P] = plane[:, at : at + P]
 
         def multiply(e, a, h, start, stop):
-            i, s = divmod(e, 2)
-            slots = slice(s * C, (s + 1) * C)
             nc.tensor.matmul_mx(
                 out=y[e, h][:],
-                lhsT=gw[i, a][:, slots].bitcast(FP8X4),
-                lhsT_scale=gs[i, a][:, slots],
+                lhsT=gw[e, a].bitcast(FP8X4),
+                lhsT_scale=gs[e, a],
                 rhs=ww[e, a, h].bitcast(FP4X4),
                 rhs_scale=w_planes[e][:, a, 512 * h : 512 * (h + 1)],
                 start=start,
@@ -209,23 +183,21 @@ def tile_moe_nxt_lin_bias_kernel(tc, x_words, x_scales, w_words, w_scales, b, wp
         def one_pass(e, a, h):
             multiply(e, a, h, False, a == PASSES - 1)
 
+        def both_halves(e, a):
+            for h in range(HALVES):
+                one_pass(e, a, h)
+
         def later_by_halves(e):
             for h in range(HALVES):
                 for a in range(1, PASSES):
                     one_pass(e, a, h)
 
-        def later_passes(e):
-            multiply(e, 1, 0, False, False)
-            multiply(e, 2, 0, False, True)
-            multiply(e, 2, 1, False, False)
-            multiply(e, 1, 1, False, True)
-
-        def gate_words(e, h, u, make_tile=vec_tile):
-            if u == 0:
-                c_rows[e, h] = make_tile([P, 2, P, 2], BF16, "c_rows%d_%d" % (e, h))
+        def gate_half(e, h, make_tile=vec_tile):
+            c_rows[e, h] = make_tile([P, 2, P, 2], BF16, "c_rows%d_%d" % (e, h))
             sums = y[e, h][:].rearrange("s (p u i) -> s u p i", u=2, i=2)
             bias = gb[e, h][:].rearrange("s (u p i) -> s u p i", u=2, i=2)
-            nc.vector.scalar_tensor_tensor(c_rows[e, h][:, u], sums[:, u], small["g"][:, e : e + 1], bias[:, u], MULT, ADD)
+            for u in range(2):
+                nc.vector.scalar_tensor_tensor(c_rows[e, h][:, u], sums[:, u], small["g"][:, e : e + 1], bias[:, u], MULT, ADD)
 
         def turn(e, h):
             pairs = c_rows[e, h][:].rearrange("s u p i -> s (u p i)").bitcast(F32)
@@ -233,9 +205,13 @@ def tile_moe_nxt_lin_bias_kernel(tc, x_words, x_scales, w_words, w_scales, b, wp
             for u in range(2):
                 nc.tensor.transpose(turned[e, h][:, u, :], pairs[:, u * P : (u + 1) * P], ident[:])
 
-        def group_c(e, h, make_tile=act_tile):
+        def group_c(e, h, make_tile=act_tile, copy=nc.scalar.copy):
             c_grouped[e, h] = make_tile([P, C, 4], BF16, "c_grouped%d_%d" % (e, h))
-            nc.scalar.copy(c_grouped[e, h][:].bitcast(F32), turned[e, h][:].rearrange("p u s -> p s u"))
+            copy(c_grouped[e, h][:].bitcast(F32), turned[e, h][:].rearrange("p u s -> p s u"))
+
+        def turn_half(e, h):
+            turn(e, h)
+            group_c(e, h)
 
         def quantize_c(e, h):
             c_codes[e, h] = vec_tile([P, C], U32, "c_codes%d_%d" % (e, h))
@@ -243,9 +219,9 @@ def tile_moe_nxt_lin_bias_kernel(tc, x_words, x_scales, w_words, w_scales, b, wp
                 c_planes[e, h] = keep_tile([P, C], U8, "c_planes%d_%d" % (e, h))
             nc.vector.quantize_mx(out=c_codes[e, h][:].bitcast(FP8X4), scales=c_planes[e, h][:], in_=c_grouped[e, h][:].rearrange("p s j -> p (s j)"))
 
-        def project_pass(sums, e, f, h, start, stop):
+        def project_pass(e, f, h, start, stop):
             nc.tensor.matmul_mx(
-                out=sums,
+                out=o[e, f],
                 lhsT=wp_codes[h, f].bitcast(FP8X4),
                 lhsT_scale=wp_planes[h, f],
                 rhs=c_codes[e, h][:].bitcast(FP8X4),
@@ -258,35 +234,28 @@ def tile_moe_nxt_lin_bias_kernel(tc, x_words, x_scales, w_words, w_scales, b, wp
             sums = bank([P, FT, C], "o")
             for f in range(FT):
                 o[e, f] = sums[:, f, :]
-                project_pass(o[e, f], e, f, 1, True, False)
-                project_pass(o[e, f], e, f, 0, False, True)
+                project_pass(e, f, 1, True, False)
+                project_pass(e, f, 0, False, True)
 
         def project_apart(e):
             for f in range(FT):
                 o[e, f] = bank([P, C], "o")[:]
-                project_pass(o[e, f], e, f, 1, True, False)
-                project_pass(o[e, f], e, f, 0, False, True)
+                project_pass(e, f, 1, True, False)
+                project_pass(e, f, 0, False, True)
 
         def project_half(e, h):
             for f in range(FT):
                 if h == 0:
                     o[e, f] = bank([P, C], "o")[:]
-                project_pass(o[e, f], e, f, h, h == 0, h == HALVES - 1)
+                project_pass(e, f, h, h == 0, h == HALVES - 1)
 
-        def leave_half(e, f, copy, make_tile):
-            o_slots[e, f] = make_tile([P, C], F32, "o_slots%d_%d" % (e, f))
-            copy(o_slots[e, f][:], o[e, f])
+        def leave_vector(e, f):
+            o_slots[e, f] = vec_tile([P, C], F32, "o_slots%d_%d" % (e, f))
+            nc.vector.tensor_copy(o_slots[e, f][:], o[e, f])
 
-        def leave_rows(e, f, make_tile=act_tile):
-            leave_half(e, f, nc.scalar.copy, make_tile)
-
-        def leave_into_pair(e, f):
-            if e % 2 == 0:
-                o_slots["pair", f] = act_tile([P, 2, C], F32, "o_pair%d" % f)
-            nc.scalar.copy(o_slots["pair", f][:, e % 2, :], o[e, f])
-
-        def scatter_pair(e, f):
-            nc.scalar.activation(windows[f][:].indirect(offsets[:, 8 * e : 8 * (e + 2)]), o_slots["pair", f][:].rearrange("p a s -> p (a s)"), COPY)
+        def leave_scalar(e, f):
+            o_slots[e, f] = act_tile([P, C], F32, "o_slots%d_%d" % (e, f))
+            nc.scalar.copy(o_slots[e, f][:], o[e, f])
 
         def scatter_vector(e, f=0):
             nc.vector.tensor_copy(windows[f][:].indirect(offsets[:, 8 * e : 8 * (e + 1)]), o_slots[e, f][:])
@@ -294,53 +263,46 @@ def tile_moe_nxt_lin_bias_kernel(tc, x_words, x_scales, w_words, w_scales, b, wp
         def scatter_scalar(e, f=1):
             nc.scalar.activation(windows[f][:].indirect(offsets[:, 8 * e : 8 * (e + 1)]), o_slots[e, f][:], COPY)
 
+        WHOLE = [[], [], [], []]
         load_bias()
-        load_gate(keep_tile)
+        load_gate()
         ident = keep.tile([P, P], F32, name="ident")
         make_identity(nc, ident[:])
         load_x(0, 1, keep_tile)
-        xs = cleared_plane(T, "xs", nc.vector.memset)
-        load_scale_rows(xs, x_scales)
-        w_planes[0] = cleared_plane(N, "ws0", nc.vector.memset)
+        xs = cleared_plane([P, PASSES, T], "xs", nc.vector.memset)
+        load_scale_rows(xs, x_scales, WHOLE)
+        w_planes[0] = cleared_plane([P, PASSES, N], "ws0", nc.vector.memset)
         load_x(1, 3, load_tile)
-        w_planes[1] = cleared_plane(N, "ws1", nc.vector.memset)
+        w_planes[1] = cleared_plane([P, PASSES, N], "ws1", nc.vector.memset)
         for e in range(2):
-            load_scale_rows(w_planes[e], w_scales[e])
+            load_scale_rows(w_planes[e], w_scales[e], WHOLE)
         small["zero"] = load_tile([P, 8], F32, "zero")
         nc.vector.memset(small["zero"][:], 0.0)
-        load_expert(0)
+        for a in range(PASSES):
+            load_w(0, a)
         load_wp(0)
         load_w(1, 0)
         load_wp(1)
 
+        spread_bias(0)
         turn_gate()
-        for e in range(E):
+        gated_bias(0)
+        for e in range(1, E):
             spread_bias(e)
             gated_bias(e)
-        gather_words(0, 0)
+        gather_words(0, 2, 0)
         for a in range(PASSES):
-            gather_scales(0, a)
-        gather_words(0, 1)
-        gather_words(0, 2)
+            gather_scales(0, 2, a)
+        gather_words(0, 2, 1)
+        gather_words(0, 2, 2)
         for a in range(PASSES):
-            gather_words(1, a)
+            gather_words(2, 4, a)
         for a in range(PASSES - 1):
-            gather_scales(1, a)
-
-        def gate_half(e, h):
-            for u in range(2):
-                gate_words(e, h, u)
-
-        def turn_half(e, h):
-            turn(e, h)
-            group_c(e, h)
-
-        def both_halves(e, a):
-            for h in range(HALVES):
-                one_pass(e, a, h)
+            gather_scales(2, 4, a)
+        gather_scales(2, 3, 2)
 
         first_pass(0)
-        later_passes(0)
+        later_by_halves(0)
         gate_half(0, 0)
         gate_half(0, 1)
         group_wp(0, nc.scalar.copy, act_tile, slice(0, M))
@@ -350,19 +312,24 @@ def tile_moe_nxt_lin_bias_kernel(tc, x_words, x_scales, w_words, w_scales, b, wp
         group_c(0, 1, load_tile)
         for f in range(FT):
             clear_window(f)
+
+        FIVE = [[], [], [], [2]]
         load_w(1, 1)
         load_w(1, 2)
         for e in range(2, E):
-            w_planes[e] = cleared_plane(N, "ws%d" % e, nc.gpsimd.memset)
-        for e in range(2, E):
-            load_scale_rows(w_planes[e], w_scales[e])
+            w_planes[e] = cleared_plane([P, PASSES, N], "ws%d" % e, nc.gpsimd.memset)
         load_w(2, 0)
+        load_scale_rows(w_planes[2], w_scales[2], FIVE)
+        load_half(2, 1, 3, 0)
+        load_half(2, 1, 2, 1)
         c_planes[0, 1] = load_tile([P, C], U8, "c_planes0_1")
-        load_w(2, 1)
+        load_half(2, 2, 3, 1)
+        load_scale_rows(w_planes[3], w_scales[3], FIVE)
         load_w(3, 0)
-        load_w(2, 2)
-        load_w(3, 1)
-        load_w(3, 2)
+        load_half(3, 1, 3, 0)
+        load_half(3, 1, 2, 1)
+        load_half(3, 2, 3, 1)
+
         quantize_wp(0, 0)
         for f in range(FT):
             group_wp(1, nc.vector.tensor_copy, vec_tile, slice(f * P, (f + 1) * P))
@@ -375,48 +342,33 @@ def tile_moe_nxt_lin_bias_kernel(tc, x_words, x_scales, w_words, w_scales, b, wp
         gate_half(1, 0)
         gate_half(1, 1)
         project(0)
-        leave_rows(0, 0)
+        leave_scalar(0, 0)
         turn_half(1, 0)
         turn_half(1, 1)
-        leave_rows(0, 1)
+        leave_scalar(0, 1)
         scatter_vector(0)
         scatter_scalar(0)
         quantize_c(1, 0)
         quantize_c(1, 1)
-        gather_scales(1, 2)
-        first_pass(2)
-        one_pass(2, 1, 0)
-        project_apart(1)
-        one_pass(2, 1, 1)
-        leave_half(1, 0, nc.vector.tensor_copy, vec_tile)
-        leave_half(1, 1, nc.scalar.copy, act_tile)
-        scatter_vector(1)
-        scatter_scalar(1)
-        first_pass(3)
-        both_halves(2, 2)
-        gate_half(2, 0)
-        gate_half(2, 1)
-        both_halves(3, 1)
-        both_halves(3, 2)
-        gate_half(3, 0)
-        gate_half(3, 1)
-        turn_half(2, 0)
-        turn_half(2, 1)
-        turn_half(3, 0)
-        turn_half(3, 1)
-        quantize_c(2, 0)
-        quantize_c(2, 1)
-        project_apart(2)
-        leave_half(2, 0, nc.scalar.copy, act_tile)
-        leave_half(2, 1, nc.scalar.copy, act_tile)
-        quantize_c(3, 0)
+        gather_scales(3, 4, 2)
+        for e in range(2, E):
+            first_pass(e)
+            later_by_halves(e)
+            gate_half(e, 0)
+            gate_half(e, 1)
+            project_apart(e - 1)
+            leave_scalar(e - 1, 0)
+            scatter_vector(e - 1)
+            turn_half(e, 0)
+            turn_half(e, 1)
+            leave_scalar(e - 1, 1)
+            scatter_scalar(e - 1)
+            quantize_c(e, 0)
+            quantize_c(e, 1)
         project_half(3, 0)
-        quantize_c(3, 1)
         project_half(3, 1)
-        scatter_vector(2)
-        scatter_scalar(2)
-        leave_half(3, 0, nc.vector.tensor_copy, vec_tile)
-        leave_half(3, 1, nc.scalar.copy, act_tile)
+        leave_vector(3, 0)
+        leave_scalar(3, 1)
         scatter_vector(3)
         scatter_scalar(3)
 

@@ -29,9 +29,9 @@ def tile_moe_nxt_lin_bias_kernel(tc, x_words, x_scales, w_words, w_scales, b, wp
     nc = tc.nc
     with ExitStack() as ctx:
         keep = ctx.enter_context(tc.tile_pool(name="keep", bufs=1))
-        loads = ctx.enter_context(tc.tile_pool(name="loads", bufs=25))
-        vec = ctx.enter_context(tc.tile_pool(name="vec", bufs=36))
-        act = ctx.enter_context(tc.tile_pool(name="act", bufs=27))
+        loads = ctx.enter_context(tc.tile_pool(name="loads", bufs=24))
+        vec = ctx.enter_context(tc.tile_pool(name="vec", bufs=37))
+        act = ctx.enter_context(tc.tile_pool(name="act", bufs=28))
         psum = ctx.enter_context(tc.psum_pool(name="psum", bufs=8))
 
         offsets = keep.tile([P, E * C // 16], U16, name="offsets")
@@ -74,9 +74,14 @@ def tile_moe_nxt_lin_bias_kernel(tc, x_words, x_scales, w_words, w_scales, b, wp
         o_slots = {}
         small = {}
 
-        def cleared_plane(shape, name, memset):
-            plane = load_tile(shape, U8, name)
+        def cleared_plane(shape, name, memset, make_tile=load_tile):
+            plane = make_tile(shape, U8, name)
             memset(plane[:].rearrange("p a n -> p (a n)").bitcast(I32), 0)
+            return plane
+
+        def copied_plane(name, zeros, make_tile=load_tile):
+            plane = make_tile([P, PASSES, N], U8, name)
+            nc.scalar.copy(plane[:].rearrange("p a n -> p (a n)").bitcast(U32), zeros[:].rearrange("p a n -> p (a n)").bitcast(U32))
             return plane
 
         def load_scale_rows(plane, scales, cuts):
@@ -118,7 +123,7 @@ def tile_moe_nxt_lin_bias_kernel(tc, x_words, x_scales, w_words, w_scales, b, wp
 
         def clear_window(f):
             windows[f] = act_tile([P, T], F32, "window%d" % f)
-            nc.scalar.activation(windows[f][:], small["zero"][:, 0:1].to_broadcast([P, T]), COPY)
+            nc.scalar.activation(windows[f][:], small["zero", f][:, 0:1].to_broadcast([P, T]), COPY)
 
         def turn_gate():
             g_turned = bank([P, C], "g_turned")
@@ -273,16 +278,32 @@ def tile_moe_nxt_lin_bias_kernel(tc, x_words, x_scales, w_words, w_scales, b, wp
         load_scale_rows(xs, x_scales, WHOLE)
         w_planes[0] = cleared_plane([P, PASSES, N], "ws0", nc.vector.memset)
         load_x(1, 3, load_tile)
-        w_planes[1] = cleared_plane([P, PASSES, N], "ws1", nc.vector.memset)
+        w_planes[3] = cleared_plane([P, PASSES, N], "ws3", nc.vector.memset, keep_tile)
+        w_planes[1] = copied_plane("ws1", w_planes[3], keep_tile)
         for e in range(2):
             load_scale_rows(w_planes[e], w_scales[e], WHOLE)
-        small["zero"] = load_tile([P, 8], F32, "zero")
-        nc.vector.memset(small["zero"][:], 0.0)
+        w_planes[2] = copied_plane("ws2", w_planes[3])
+        small["zero", 0] = load_tile([P, 8], F32, "zero0")
+        nc.scalar.copy(small["zero", 0][:].bitcast(U32), w_planes[3][:, 0, 0:32].bitcast(U32))
+        small["zero", 1] = small["zero", 0]
         for a in range(PASSES):
             load_w(0, a)
         load_wp(0)
         load_w(1, 0)
         load_wp(1)
+        load_w(1, 1)
+        load_w(1, 2)
+        load_w(2, 0)
+        load_scale_rows(w_planes[2], w_scales[2], [[], [], [], [2]])
+        load_half(2, 1, 3, 0)
+        load_half(2, 1, 2, 1)
+        load_half(2, 2, 3, 1)
+        load_scale_rows(w_planes[3], w_scales[3], [[], [], [], [2]])
+        load_w(3, 0)
+        load_half(3, 1, 3, 0)
+        load_half(3, 1, 2, 1)
+        c_planes[1, 1] = load_tile([P, C], U8, "c_planes1_1")
+        load_half(3, 2, 3, 1)
 
         spread_bias(0)
         turn_gate()
@@ -291,8 +312,9 @@ def tile_moe_nxt_lin_bias_kernel(tc, x_words, x_scales, w_words, w_scales, b, wp
             spread_bias(e)
             gated_bias(e)
         gather_words(0, 2, 0)
-        for a in range(PASSES):
-            gather_scales(0, 2, a)
+        gather_scales(0, 2, 0)
+        gather_scales(0, 1, 1)
+        gather_scales(0, 2, 2)
         gather_words(0, 2, 1)
         gather_words(0, 2, 2)
         for a in range(PASSES):
@@ -305,30 +327,13 @@ def tile_moe_nxt_lin_bias_kernel(tc, x_words, x_scales, w_words, w_scales, b, wp
         later_by_halves(0)
         gate_half(0, 0)
         gate_half(0, 1)
+        gather_scales(1, 2, 1)
         group_wp(0, nc.scalar.copy, act_tile, slice(0, M))
         first_pass(1)
         turn_half(0, 0)
-        turn(0, 1)
-        group_c(0, 1, load_tile)
+        turn_half(0, 1)
         for f in range(FT):
             clear_window(f)
-
-        FIVE = [[], [], [], [2]]
-        load_w(1, 1)
-        load_w(1, 2)
-        for e in range(2, E):
-            w_planes[e] = cleared_plane([P, PASSES, N], "ws%d" % e, nc.gpsimd.memset)
-        load_w(2, 0)
-        load_scale_rows(w_planes[2], w_scales[2], FIVE)
-        load_half(2, 1, 3, 0)
-        load_half(2, 1, 2, 1)
-        c_planes[0, 1] = load_tile([P, C], U8, "c_planes0_1")
-        load_half(2, 2, 3, 1)
-        load_scale_rows(w_planes[3], w_scales[3], FIVE)
-        load_w(3, 0)
-        load_half(3, 1, 3, 0)
-        load_half(3, 1, 2, 1)
-        load_half(3, 2, 3, 1)
 
         quantize_wp(0, 0)
         for f in range(FT):

@@ -80,7 +80,7 @@ def tile_moe_nxt_lin_bias_kernel(tc, x_words, x_scales, w_words, w_scales, b, wp
             return plane
 
         def copied_plane(name, zeros, make_tile=load_tile):
-            plane = make_tile([P, PASSES, N], U8, name)
+            plane = make_tile(zeros.shape, U8, name)
             nc.scalar.copy(plane[:].rearrange("p a n -> p (a n)").bitcast(U32), zeros[:].rearrange("p a n -> p (a n)").bitcast(U32))
             return plane
 
@@ -113,13 +113,13 @@ def tile_moe_nxt_lin_bias_kernel(tc, x_words, x_scales, w_words, w_scales, b, wp
             wp_raw[h] = load_tile([P, 4, M], F32, "wp_raw%d" % h)
             nc.sync.dma_start(wp_raw[h][:], wp[512 * h : 512 * (h + 1)].rearrange("(p j) f -> p j f", j=4))
 
-        def load_bias():
+        def load_bias(queue=nc.scalar):
             small["b"] = keep.tile([P, HALVES, 4, E], F32, name="b_col")
-            nc.scalar.dma_start(small["b"][:], b.rearrange("(h p j) e -> p h j e", h=HALVES, j=4))
+            queue.dma_start(small["b"][:], b.rearrange("(h p j) e -> p h j e", h=HALVES, j=4))
 
-        def load_gate():
+        def load_gate(queue=nc.scalar):
             small["g_rows"] = keep_tile([P, C], F32, "g_rows")
-            nc.scalar.dma_start(small["g_rows"][:], gate.rearrange("r (e s) -> (r e) s", s=C)[0:P])
+            queue.dma_start(small["g_rows"][:], gate.rearrange("r (e s) -> (r e) s", s=C)[0:P])
 
         def clear_window(f):
             windows[f] = act_tile([P, T], F32, "window%d" % f)
@@ -294,7 +294,7 @@ def tile_moe_nxt_lin_bias_kernel(tc, x_words, x_scales, w_words, w_scales, b, wp
         load_w(1, 1)
         load_w(1, 2)
         load_w(2, 0)
-        load_scale_rows(w_planes[2], w_scales[2], [[], [], [], [2]])
+        load_scale_rows(w_planes[2], w_scales[2], [[], [], [2], [2]])
         load_half(2, 1, 3, 0)
         load_half(2, 1, 2, 1)
         load_half(2, 2, 3, 1)
@@ -312,16 +312,17 @@ def tile_moe_nxt_lin_bias_kernel(tc, x_words, x_scales, w_words, w_scales, b, wp
             spread_bias(e)
             gated_bias(e)
         gather_words(0, 2, 0)
+        gather_words(2, 4, 0)
         gather_scales(0, 2, 0)
         gather_scales(0, 1, 1)
         gather_scales(0, 2, 2)
         gather_words(0, 2, 1)
         gather_words(0, 2, 2)
-        for a in range(PASSES):
+        for a in range(1, PASSES):
             gather_words(2, 4, a)
-        for a in range(PASSES - 1):
-            gather_scales(2, 4, a)
-        gather_scales(2, 3, 2)
+        gather_scales(2, 4, 0)
+        gather_scales(3, 4, 1)
+        gather_scales(2, 4, 2)
 
         first_pass(0)
         later_by_halves(0)
@@ -344,28 +345,22 @@ def tile_moe_nxt_lin_bias_kernel(tc, x_words, x_scales, w_words, w_scales, b, wp
         both_halves(1, 1)
         both_halves(1, 2)
         quantize_c(0, 1)
-        gate_half(1, 0)
-        gate_half(1, 1)
-        project(0)
-        leave_scalar(0, 0)
-        turn_half(1, 0)
-        turn_half(1, 1)
-        leave_scalar(0, 1)
-        scatter_vector(0)
-        scatter_scalar(0)
-        quantize_c(1, 0)
-        quantize_c(1, 1)
-        gather_scales(3, 4, 2)
-        for e in range(2, E):
-            first_pass(e)
-            later_by_halves(e)
+        for e in range(1, E):
+            if e > 1:
+                later_by_halves(e)
             gate_half(e, 0)
             gate_half(e, 1)
             project_apart(e - 1)
             leave_scalar(e - 1, 0)
+            if e in (1,):
+                first_pass(e + 1)
+            if e == 1:
+                gather_scales(2, 3, 1)
             scatter_vector(e - 1)
             turn_half(e, 0)
             turn_half(e, 1)
+            if e + 1 < E and e not in (1,):
+                first_pass(e + 1)
             leave_scalar(e - 1, 1)
             scatter_scalar(e - 1)
             quantize_c(e, 0)

@@ -242,11 +242,14 @@ def tile_moe_nxt_lin_bias_kernel(tc, x_words, x_scales, w_words, w_scales, b, wp
                 project_pass(e, f, 1, True, False)
                 project_pass(e, f, 0, False, True)
 
+        def project_block(e, f):
+            o[e, f] = bank([P, C], "o")[:]
+            project_pass(e, f, 1, True, False)
+            project_pass(e, f, 0, False, True)
+
         def project_apart(e):
             for f in range(FT):
-                o[e, f] = bank([P, C], "o")[:]
-                project_pass(e, f, 1, True, False)
-                project_pass(e, f, 0, False, True)
+                project_block(e, f)
 
         def project_half(e, h):
             for f in range(FT):
@@ -295,13 +298,13 @@ def tile_moe_nxt_lin_bias_kernel(tc, x_words, x_scales, w_words, w_scales, b, wp
         load_w(1, 2)
         load_w(2, 0)
         load_scale_rows(w_planes[2], w_scales[2], [[], [], [2], [2]])
-        load_half(2, 1, 3, 0)
-        load_half(2, 1, 2, 1)
+        load_w(2, 1)
+        load_half(2, 2, 3, 0)
         load_half(2, 2, 3, 1)
         load_scale_rows(w_planes[3], w_scales[3], [[], [], [], [2]])
         load_w(3, 0)
-        load_half(3, 1, 3, 0)
-        load_half(3, 1, 2, 1)
+        load_w(3, 1)
+        load_half(3, 2, 3, 0)
         c_planes[1, 1] = load_tile([P, C], U8, "c_planes1_1")
         load_half(3, 2, 3, 1)
 
@@ -350,7 +353,9 @@ def tile_moe_nxt_lin_bias_kernel(tc, x_words, x_scales, w_words, w_scales, b, wp
                 later_by_halves(e)
             gate_half(e, 0)
             gate_half(e, 1)
-            project_apart(e - 1)
+            project_block(e - 1, 0)
+            if e < 3:
+                project_block(e - 1, 1)
             leave_scalar(e - 1, 0)
             if e in (1,):
                 first_pass(e + 1)
@@ -361,6 +366,8 @@ def tile_moe_nxt_lin_bias_kernel(tc, x_words, x_scales, w_words, w_scales, b, wp
             turn_half(e, 1)
             if e + 1 < E and e not in (1,):
                 first_pass(e + 1)
+            if e == 3:
+                project_block(2, 1)
             leave_scalar(e - 1, 1)
             scatter_scalar(e - 1)
             quantize_c(e, 0)

from contextlib import ExitStack

import concourse.mybir as mybir
from concourse.masks import make_identity

K, T, E, C, N, M = 1536, 640, 4, 128, 1024, 256
P = 128
PASSES = K // 512
HALVES = N // 512
FT = M // P

FLOPS = 2 * K * N * E * C + 2 * N * M * T
BYTES = 983040 + 30720 + 3145728 + 196608 + 16384 + 1048576 + 2048 + 8192 + 655360

F32 = mybir.dt.float32
BF16 = mybir.dt.bfloat16
I32 = mybir.dt.int32
U32 = mybir.dt.uint32
U16 = mybir.dt.uint16
U8 = mybir.dt.uint8
FP8X4 = mybir.dt.float8_e4m3fn_x4
FP4X4 = mybir.dt.float4_e2m1fn_x4
MULT = mybir.AluOpType.mult
ADD = mybir.AluOpType.add
COPY = mybir.ActivationFunctionType.Copy


def tile_moe_nxt_lin_bias_kernel(tc, x_words, x_scales, w_words, w_scales, b, wp, gate, offs, out):
    nc = tc.nc
    with ExitStack() as ctx:
        keep = ctx.enter_context(tc.tile_pool(name="keep", bufs=1))
        loads = ctx.enter_context(tc.tile_pool(name="loads", bufs=24))
        vec = ctx.enter_context(tc.tile_pool(name="vec", bufs=37))
        act = ctx.enter_context(tc.tile_pool(name="act", bufs=28))
        psum = ctx.enter_context(tc.psum_pool(name="psum", bufs=8))

        offsets = keep.tile([P, E * C // 16], U16, name="offsets")
        nc.sync.dma_start(offsets[:], offs)

        def keep_tile(shape, dtype, name):
            return keep.tile(shape, dtype, name=name, align_bytes=64)

        def load_tile(shape, dtype, name):
            return loads.tile(shape, dtype, name=name, tag="load", align_bytes=256)

        def vec_tile(shape, dtype, name):
            return vec.tile(shape, dtype, name=name, tag="vec", align_bytes=64)

        def act_tile(shape, dtype, name):
            return act.tile(shape, dtype, name=name, tag="act", align_bytes=64)

        def bank(shape, name):
            return psum.tile(shape, F32, name=name, tag="bank")

        x_windows = {}
        ww = {}
        wp_raw = {}
        w_planes = {}
        windows = {}
        gw = {}
        gs = {}
        gb = {}
        spread = {}
        wp_grouped = {}
        wp_codes = {}
        wp_planes = {}
        y = {}
        c_rows = {}
        turned = {}
        c_grouped = {}
        c_codes = {}
        c_planes = {}
        o = {}
        o_slots = {}
        small = {}

        def cleared_plane(shape, name, memset, make_tile=load_tile):
            plane = make_tile(shape, U8, name)
            memset(plane[:].rearrange("p a n -> p (a n)").bitcast(I32), 0)
            return plane

        def copied_plane(name, zeros, make_tile=load_tile):
            plane = make_tile(zeros.shape, U8, name)
            nc.scalar.copy(plane[:].rearrange("p a n -> p (a n)").bitcast(U32), zeros[:].rearrange("p a n -> p (a n)").bitcast(U32))
            return plane

        def load_scale_rows(plane, scales, cuts):
            rows = scales.rearrange("a (q r) n -> r q a n", r=4)
            for r in range(4):
                edges = [0] + cuts[r] + [plane.shape[1]]
                for first, last in zip(edges, edges[1:]):
                    nc.sync.dma_start(plane[r:P:32, first:last].bitcast(I32), rows[r][:, first:last].bitcast(I32))

        def load_x(first, last, make_tile):
            tile = make_tile([P, last - first, T], I32, "xw%d" % first)
            nc.sync.dma_start(tile[:], x_words[first:last].rearrange("a p t r -> p a (t r)").bitcast(I32))
            for a in range(first, last):
                x_windows[a] = tile[:, a - first, :]

        def load_w(e, a):
            tile = load_tile([P, 2 * N], U8, "ww%d_%d" % (e, a))
            nc.sync.dma_start(tile[:].bitcast(I32), w_words[e, a].bitcast(I32))
            for h in range(HALVES):
                ww[e, a, h] = tile[:, N * h : N * (h + 1)]

        def load_half(e, first, last, h):
            tile = load_tile([P, last - first, N], U8, "ww%d_%d_%d" % (e, first, h))
            nc.sync.dma_start(tile[:].bitcast(I32), w_words[e, first:last].rearrange("a p n -> p a n")[:, :, N * h : N * (h + 1)].bitcast(I32))
            for a in range(first, last):
                ww[e, a, h] = tile[:, a - first, :]

        def load_wp(h):
            wp_raw[h] = load_tile([P, 4, M], F32, "wp_raw%d" % h)
            nc.sync.dma_start(wp_raw[h][:], wp[512 * h : 512 * (h + 1)].rearrange("(p j) f -> p j f", j=4))

        def load_bias(queue=nc.scalar):
            small["b"] = keep.tile([P, HALVES, 4, E], F32, name="b_col")
            queue.dma_start(small["b"][:], b.rearrange("(h p j) e -> p h j e", h=HALVES, j=4))

        def load_gate(queue=nc.scalar):
            small["g_rows"] = keep_tile([P, C], F32, "g_rows")
            queue.dma_start(small["g_rows"][:], gate.rearrange("r (e s) -> (r e) s", s=C)[0:P])

        def clear_window(f):
            windows[f] = act_tile([P, T], F32, "window%d" % f)
            nc.scalar.activation(windows[f][:], small["zero", f][:, 0:1].to_broadcast([P, T]), COPY)

        def turn_gate():
            g_turned = bank([P, C], "g_turned")
            nc.tensor.transpose(g_turned[:], small["g_rows"][:], ident[:])
            small["g"] = act_tile([P, E], F32, "g_col")
            nc.scalar.copy(small["g"][:], g_turned[:, 0:E])

        def gather_scales(first, last, a):
            tile = vec_tile([P, (last - first) * C], U8, "gs%d_%d" % (first, a))
            nc.vector.tensor_copy(tile[:], xs[:, a, :].indirect(offsets[:, 8 * first : 8 * last]))
            for e in range(first, last):
                gs[e, a] = tile[:, (e - first) * C : (e - first + 1) * C]

        def gather_words(first, last, a):
            tile = vec_tile([P, (last - first) * C], U32, "gw%d_%d" % (first, a))
            nc.vector.tensor_copy(tile[:], x_windows[a].bitcast(U32).indirect(offsets[:, 8 * first : 8 * last]))
            for e in range(first, last):
                gw[e, a] = tile[:, (e - first) * C : (e - first + 1) * C]

        def spread_bias(e):
            for h in range(HALVES):
                spread[e, h] = bank([P, 4, P], "spread")
                for j in range(4):
                    nc.tensor.transpose(spread[e, h][:, j, :], small["b"][:, h, j, e : e + 1].to_broadcast([P, P]), ident[:])

        def gated_bias(e):
            for h in range(HALVES):
                gb[e, h] = act_tile([P, 512], F32, "gb%d_%d" % (e, h))
                nc.scalar.activation(gb[e, h][:].rearrange("s (u p i) -> s u p i", u=2, i=2), spread[e, h][:].rearrange("s (u i) p -> s u p i", u=2), COPY, scale=small["g"][:, e : e + 1])

        def group_wp(h, copy, make_tile, cols):
            grouped = make_tile([P, cols.stop - cols.start, 4], BF16, "wp_grouped%d_%d" % (h, cols.start))
            copy(grouped[:].rearrange("p (c i) j -> p c j i", i=4), wp_raw[h][:, :, cols].rearrange("p j (c i) -> p c j i", i=4))
            wp_grouped[h, cols.start] = grouped

        def quantize_wp(h, first):
            grouped = wp_grouped[h, first]
            width = grouped.shape[1]
            codes = vec_tile([P, width], U32, "wp_codes%d_%d" % (h, first))
            plane = keep_tile([P, width], U8, "wp_planes%d_%d" % (h, first))
            nc.vector.quantize_mx(out=codes[:].bitcast(FP8X4), scales=plane[:], in_=grouped[:].rearrange("p f j -> p (f j)"))
            for at in range(0, width, P):
                wp_codes[h, (first + at) // P] = codes[:, at : at + P]
                wp_planes[h, (first + at) // P] = plane[:, at : at + P]

        def multiply(e, a, h, start, stop):
            nc.tensor.matmul_mx(
                out=y[e, h][:],
                lhsT=gw[e, a].bitcast(FP8X4),
                lhsT_scale=gs[e, a],
                rhs=ww[e, a, h].bitcast(FP4X4),
                rhs_scale=w_planes[e][:, a, 512 * h : 512 * (h + 1)],
                start=start,
                stop=stop,
            )

        def first_pass(e):
            for h in range(HALVES):
                y[e, h] = bank([P, 512], "y")
                multiply(e, 0, h, True, False)

        def one_pass(e, a, h):
            multiply(e, a, h, False, a == PASSES - 1)

        def both_halves(e, a):
            for h in range(HALVES):
                one_pass(e, a, h)

        def later_by_halves(e):
            for h in range(HALVES):
                for a in range(1, PASSES):
                    one_pass(e, a, h)

        def gate_half(e, h, make_tile=vec_tile):
            c_rows[e, h] = make_tile([P, 2, P, 2], BF16, "c_rows%d_%d" % (e, h))
            sums = y[e, h][:].rearrange("s (p u i) -> s u p i", u=2, i=2)
            bias = gb[e, h][:].rearrange("s (u p i) -> s u p i", u=2, i=2)
            for u in range(2):
                nc.vector.scalar_tensor_tensor(c_rows[e, h][:, u], sums[:, u], small["g"][:, e : e + 1], bias[:, u], MULT, ADD)

        def turn(e, h):
            pairs = c_rows[e, h][:].rearrange("s u p i -> s (u p i)").bitcast(F32)
            turned[e, h] = bank([P, 2, P], "turned")
            for u in range(2):
                nc.tensor.transpose(turned[e, h][:, u, :], pairs[:, u * P : (u + 1) * P], ident[:])

        def group_c(e, h, make_tile=act_tile, copy=nc.scalar.copy):
            c_grouped[e, h] = make_tile([P, C, 4], BF16, "c_grouped%d_%d" % (e, h))
            copy(c_grouped[e, h][:].bitcast(F32), turned[e, h][:].rearrange("p u s -> p s u"))

        def turn_half(e, h):
            turn(e, h)
            group_c(e, h)

        def quantize_c(e, h):
            c_codes[e, h] = vec_tile([P, C], U32, "c_codes%d_%d" % (e, h))
            if (e, h) not in c_planes:
                c_planes[e, h] = keep_tile([P, C], U8, "c_planes%d_%d" % (e, h))
            nc.vector.quantize_mx(out=c_codes[e, h][:].bitcast(FP8X4), scales=c_planes[e, h][:], in_=c_grouped[e, h][:].rearrange("p s j -> p (s j)"))

        def project_pass(e, f, h, start, stop):
            nc.tensor.matmul_mx(
                out=o[e, f],
                lhsT=wp_codes[h, f].bitcast(FP8X4),
                lhsT_scale=wp_planes[h, f],
                rhs=c_codes[e, h][:].bitcast(FP8X4),
                rhs_scale=c_planes[e, h][:],
                start=start,
                stop=stop,
            )

        def project(e):
            sums = bank([P, FT, C], "o")
            for f in range(FT):
                o[e, f] = sums[:, f, :]
                project_pass(e, f, 1, True, False)
                project_pass(e, f, 0, False, True)

        def project_block(e, f):
            o[e, f] = bank([P, C], "o")[:]
            project_pass(e, f, 1, True, False)
            project_pass(e, f, 0, False, True)

        def project_apart(e):
            for f in range(FT):
                project_block(e, f)

        def project_half(e, h):
            for f in range(FT):
                if h == 0:
                    o[e, f] = bank([P, C], "o")[:]
                project_pass(e, f, h, h == 0, h == HALVES - 1)

        def leave_vector(e, f):
            o_slots[e, f] = vec_tile([P, C], F32, "o_slots%d_%d" % (e, f))
            nc.vector.tensor_copy(o_slots[e, f][:], o[e, f])

        def leave_scalar(e, f):
            o_slots[e, f] = act_tile([P, C], F32, "o_slots%d_%d" % (e, f))
            nc.scalar.copy(o_slots[e, f][:], o[e, f])

        def scatter_vector(e, f=0):
            nc.vector.tensor_copy(windows[f][:].indirect(offsets[:, 8 * e : 8 * (e + 1)]), o_slots[e, f][:])

        def scatter_scalar(e, f=1):
            nc.scalar.activation(windows[f][:].indirect(offsets[:, 8 * e : 8 * (e + 1)]), o_slots[e, f][:], COPY)

        WHOLE = [[], [], [], []]
        load_bias()
        load_gate()
        ident = keep.tile([P, P], F32, name="ident")
        make_identity(nc, ident[:])
        load_x(0, 1, keep_tile)
        xs = cleared_plane([P, PASSES, T], "xs", nc.vector.memset)
        load_scale_rows(xs, x_scales, WHOLE)
        w_planes[0] = cleared_plane([P, PASSES, N], "ws0", nc.vector.memset)
        load_x(1, 3, load_tile)
        w_planes[3] = cleared_plane([P, PASSES, N], "ws3", nc.vector.memset, keep_tile)
        w_planes[1] = copied_plane("ws1", w_planes[3], keep_tile)
        for e in range(2):
            load_scale_rows(w_planes[e], w_scales[e], WHOLE)
        w_planes[2] = copied_plane("ws2", w_planes[3])
        small["zero", 0] = load_tile([P, 8], F32, "zero0")
        nc.scalar.copy(small["zero", 0][:].bitcast(U32), w_planes[3][:, 0, 0:32].bitcast(U32))
        small["zero", 1] = small["zero", 0]
        for a in range(PASSES):
            load_w(0, a)
        load_wp(0)
        load_w(1, 0)
        load_wp(1)
        load_w(1, 1)
        load_w(1, 2)
        load_w(2, 0)
        load_scale_rows(w_planes[2], w_scales[2], [[], [], [2], [2]])
        load_w(2, 1)
        load_half(2, 2, 3, 0)
        load_half(2, 2, 3, 1)
        load_scale_rows(w_planes[3], w_scales[3], [[], [], [], [2]])
        load_w(3, 0)
        load_w(3, 1)
        load_half(3, 2, 3, 0)
        c_planes[1, 1] = load_tile([P, C], U8, "c_planes1_1")
        load_half(3, 2, 3, 1)

        spread_bias(0)
        turn_gate()
        gated_bias(0)
        for e in range(1, E):
            spread_bias(e)
            gated_bias(e)
        gather_words(0, 2, 0)
        gather_words(2, 4, 0)
        gather_scales(0, 2, 0)
        gather_scales(0, 1, 1)
        gather_scales(0, 2, 2)
        gather_words(0, 2, 1)
        gather_words(0, 2, 2)
        for a in range(1, PASSES):
            gather_words(2, 4, a)
        gather_scales(2, 4, 0)
        gather_scales(3, 4, 1)
        gather_scales(2, 4, 2)

        first_pass(0)
        later_by_halves(0)
        gate_half(0, 0)
        gate_half(0, 1)
        gather_scales(1, 2, 1)
        group_wp(0, nc.scalar.copy, act_tile, slice(0, M))
        first_pass(1)
        turn_half(0, 0)
        turn_half(0, 1)
        for f in range(FT):
            clear_window(f)

        quantize_wp(0, 0)
        for f in range(FT):
            group_wp(1, nc.vector.tensor_copy, vec_tile, slice(f * P, (f + 1) * P))
        quantize_c(0, 0)
        for f in range(FT):
            quantize_wp(1, f * P)
        both_halves(1, 1)
        both_halves(1, 2)
        quantize_c(0, 1)
        for e in range(1, E):
            if e > 1:
                later_by_halves(e)
            gate_half(e, 0)
            gate_half(e, 1)
            project_block(e - 1, 0)
            if e < 3:
                project_block(e - 1, 1)
            leave_scalar(e - 1, 0)
            if e in (1,):
                first_pass(e + 1)
            if e == 1:
                gather_scales(2, 3, 1)
            scatter_vector(e - 1)
            turn_half(e, 0)
            turn_half(e, 1)
            if e + 1 < E and e not in (1,):
                first_pass(e + 1)
            if e == 3:
                project_block(2, 1)
            leave_scalar(e - 1, 1)
            scatter_scalar(e - 1)
            quantize_c(e, 0)
            quantize_c(e, 1)
        project_half(3, 0)
        project_half(3, 1)
        leave_vector(3, 0)
        leave_scalar(3, 1)
        scatter_vector(3)
        scatter_scalar(3)

        nc.sync.dma_start(out[0:P, :], windows[0][:])
        nc.scalar.dma_start(out[P : 2 * P, :], windows[1][:])
